import numpy as np
import ml_dtypes


def mxq(x, axis, fmt="e4m3"):
    dtype, down = {"e4m3": (ml_dtypes.float8_e4m3fn, 7), "e5m2": (ml_dtypes.float8_e5m2, 14)}[fmt]
    v = np.moveaxis(np.asarray(x, np.float32).astype(ml_dtypes.bfloat16).astype(np.float64), axis, -1)
    blocks = v.reshape(v.shape[:-1] + (-1, 32))
    amax = np.abs(blocks).max(-1, keepdims=True)
    byte = np.maximum(np.where(amax > 0, np.frexp(amax)[1] - 1 + 127, 0) - down, 1)
    scale = np.exp2(byte - 127.0)
    codes = (blocks / scale).astype(np.float32).astype(dtype).astype(np.float64)
    return np.moveaxis((codes * scale).reshape(v.shape), -1, axis)


WIDE = False


def mx_kscale(k):
    if not WIDE:
        return np.ones(k)
    levels = np.array([10, -10, 5, -5, 0])
    if k % 512:
        return np.exp2(np.random.permutation(np.resize(levels, k // 32))).repeat(32)
    a = np.empty((k // 512, 16))
    for p in range(k // 512):
        a[p, :8] = np.random.permutation(np.resize(levels, 8))
        for g in range(8):
            far = levels[np.abs(levels - a[p, g]) >= 10]
            a[p, g + 8] = far[np.random.randint(len(far))]
    return np.exp2(a.ravel()).repeat(32)


def f64(x):
    return np.asarray(x).astype(np.float64)


def striped(idx):
    return np.tile(idx.reshape(-1, 16).T, (8, 1)).astype(np.uint16)


def unstriped(offs):
    return offs[:16].T.reshape(-1).astype(np.int64)


E2M1 = np.array([0.0, 0.5, 1.0, 1.5, 2.0, 3.0, 4.0, 6.0, -0.0, -0.5, -1.0, -1.5, -2.0, -3.0, -4.0, -6.0])


def pack_weight(w, fmt):
    k, n = w.shape
    w = f64(np.asarray(w, np.float32).astype(ml_dtypes.bfloat16)).reshape(k // 32, 32, n)
    amax = np.abs(w).max(1)
    if fmt == "e4m3":
        byte = np.frexp(amax)[1] - 1 + 127 - 7
    else:
        mant, ex = np.frexp(amax / 6.0)
        byte = np.where(mant > 0.5, ex, ex - 1) + 127
    byte = np.clip(np.where(amax > 0, byte, 1), 1, 254)
    scaled = (w * np.exp2(127.0 - byte)[:, None, :]).reshape(k, n).astype(np.float32)
    by_word = np.ascontiguousarray(scaled.reshape(k // 512, 128, 4, n).transpose(0, 1, 3, 2))
    if fmt == "e4m3":
        words = by_word.astype(ml_dtypes.float8_e4m3fn).view(np.uint8)
    else:
        c = by_word.astype(ml_dtypes.float4_e2m1fn).view(np.uint8) & 0xF
        words = (c[..., 0::2] | (c[..., 1::2] << 4)).reshape(k // 512, 128, 2 * n)
    return np.ascontiguousarray(words), np.ascontiguousarray(byte.astype(np.uint8).reshape(k // 512, 16, n))


def unpack_weight(words, scales, fmt):
    g, _, n = scales.shape
    words = np.ascontiguousarray(words).reshape(g, 128, n, -1)
    if fmt == "e4m3":
        vals = words.view(ml_dtypes.float8_e4m3fn).astype(np.float64)
    else:
        nib = np.empty((g, 128, n, 4), np.uint8)
        nib[..., 0::2] = words & 0xF
        nib[..., 1::2] = words >> 4
        vals = E2M1[nib]
    vals = vals * np.repeat(np.exp2(scales.astype(np.float64) - 127.0), 8, axis=1)[..., None]
    return vals.transpose(0, 1, 3, 2).reshape(g * 512, n)


def gelu(v):
    return 0.5 * v * (1.0 + np.tanh(np.sqrt(2.0 / np.pi) * (v + 0.044715 * v**3)))


K, H, N, T, S, T2 = 1024, 512, 512, 4096, 1024, 2048


def setup_inputs():
    n = np.random.standard_normal
    s = mx_kscale(K)[:, None]
    u = mx_kscale(H)[:, None]
    v = n((K, T)) * np.exp(0.4 * n((1, T))) * s
    tab_words, tab_scales = pack_weight(v, "e4m3")
    w1 = n((K, H)) / np.sqrt(K) / s * u.T
    w4_words, w4_scales = pack_weight(n((K, H)) / np.sqrt(K) / s * u.T, "e2m1")
    w2 = np.exp(1.5 * n((H, N))) / (3.0 * H) / (u * u)
    return {
        "tab_words": tab_words, "tab_scales": tab_scales,
        "offs": striped(np.random.permutation(T)[:S]),
        "w1": w1.astype(np.float32),
        "w4_words": w4_words, "w4_scales": w4_scales,
        "w2": w2.astype(np.float32),
        "wgo": np.exp(0.3 * n((128, S))).astype(np.float32),
        "offs2": striped(np.random.permutation(T2)[:S]),
    }


def reference(tab_words, tab_scales, offs, w1, w4_words, w4_scales, w2, wgo, offs2):
    v = unpack_weight(tab_words, tab_scales, "e4m3")[:, unstriped(offs)]
    w4 = unpack_weight(w4_words, w4_scales, "e2m1")
    a = mxq(f64(w1), 0, "e4m3").T @ v
    b = w4.T @ v
    h = np.square(a - b)
    x = mxq(f64(w2), 0, "e4m3").T @ mxq(h, 0, "e4m3")
    y = np.sqrt(1.0 + x)
    out = np.zeros((N, T2))
    out[:, unstriped(offs2)] = np.tile(f64(wgo), (N // 128, 1)) * y
    return out

@@ -1,0 +1,222 @@
+from contextlib import ExitStack
+
+import concourse.mybir as mybir
+
+K, H, N, T, S, T2 = 1024, 512, 512, 4096, 1024, 2048
+FLOPS = 2 * K * H * S * 2 + 2 * H * N * S
+
+F32 = mybir.dt.float32
+BF16 = mybir.dt.bfloat16
+I32 = mybir.dt.int32
+U32 = mybir.dt.uint32
+U16 = mybir.dt.uint16
+U8 = mybir.dt.uint8
+FP8X4 = mybir.dt.float8_e4m3fn_x4
+FP4X4 = mybir.dt.float4_e2m1fn_x4
+ACT = mybir.ActivationFunctionType
+MULT = mybir.AluOpType.mult
+
+P = 128
+PACK = 4
+K_PASS = P * PACK
+PASSES = K // K_PASS
+COLS = 128
+CHUNK = 256
+HALF = 512
+AL = 64
+
+
+def tile_list_replay_huber_novelty_kernel(
+    tc, tab_words, tab_scales, offs, w1, w4_words, w4_scales, w2, wgo, offs2, out
+):
+    nc = tc.nc
+    with ExitStack() as ctx:
+        lists = ctx.enter_context(tc.tile_pool(name="lists", bufs=1))
+        keep = ctx.enter_context(tc.tile_pool(name="keep", bufs=1))
+        ring = ctx.enter_context(tc.tile_pool(name="ring", bufs=3))
+        psum1 = ctx.enter_context(tc.psum_pool(name="psum1", bufs=4))
+        psum2 = ctx.enter_context(tc.psum_pool(name="psum2", bufs=4))
+
+        idx = lists.tile([P, S // 16], U16, name="idx")
+        idx2 = lists.tile([P, S // 16], U16, name="idx2")
+
+        tab_sc = keep.tile([P, T // 4], I32, name="tab_sc", align_bytes=AL)
+        w4_sc_raw = keep.tile([P, PASSES, H // 4], I32, name="w4_sc_raw", align_bytes=AL)
+        v_sc1 = keep.tile([P, S // 4], I32, name="v_sc1", align_bytes=AL)
+        ones = keep.tile([P, 1], F32, name="ones")
+        warm = keep.tile([P, 1], F32, name="warm")
+        nc.vector.memset(w4_sc_raw[:], 0)
+        nc.vector.memset(tab_sc[:], 0)
+        nc.vector.memset(v_sc1[:], 0)
+        nc.vector.memset(ones[:], 1.0)
+        nc.scalar.activation(warm[:], ones[:], ACT.Sqrt, bias=ones[:])
+
+        for q in range(4):
+            nc.scalar.dma_start(
+                w4_sc_raw[32 * q : 32 * q + 4, :, :],
+                w4_scales[:, 4 * q : 4 * q + 4, :].rearrange("a r c -> r a c").bitcast(I32),
+            )
+        nc.sync.dma_start(idx[:], offs)
+        w1_raw = []
+        for a in range(PASSES):
+            raw = keep.tile([P, PACK, H], F32, name="w1_raw%d" % a, tag="big%d" % a, align_bytes=AL)
+            nc.sync.dma_start(raw[:], w1[a * K_PASS : (a + 1) * K_PASS, :].rearrange("(p i) c -> p i c", i=PACK))
+            w1_raw.append(raw)
+        w4_raw = keep.tile([P, PASSES, H // 2], I32, name="w4_raw", align_bytes=AL)
+        nc.sync.dma_start(w4_raw[:], w4_words.rearrange("a p c -> p a c").bitcast(I32))
+        tab = []
+        for a in range(PASSES):
+            words = keep.tile([P, T], I32, name="tab%d" % a, tag="big%d" % (2 + a), align_bytes=AL)
+            nc.sync.dma_start(words[:], tab_words[a].rearrange("p t i -> p (t i)").bitcast(I32))
+            tab.append(words)
+        w2_raw = keep.tile([P, PACK, N], F32, name="w2_raw", align_bytes=AL)
+        w2_rows = w2.rearrange("(q t m) n -> t q m n", t=PACK, m=8)
+        for t in range(PACK):
+            nc.sync.dma_start(w2_raw[:, t, :], w2_rows[t])
+        wgo_sb = keep.tile([P, S], F32, name="wgo_sb", align_bytes=AL)
+        nc.sync.dma_start(wgo_sb[:], wgo)
+        nc.sync.dma_start(idx2[:], offs2)
+
+        for q in range(4):
+            nc.gpsimd.dma_start(tab_sc[32 * q : 32 * q + 8, :], tab_scales[:, 4 * q : 4 * q + 4, :].bitcast(I32))
+
+        v_sc = keep.tile([P, S // 4], I32, name="v_sc", align_bytes=AL)
+        nc.vector.tensor_copy(v_sc[:].bitcast(U8), tab_sc[:].bitcast(U8).indirect(idx[:]))
+
+        w1_bf = keep.tile([P, PASSES, PACK, COLS * PACK], BF16, name="w1_bf", align_bytes=AL)
+        w1_q = keep.tile([P, PASSES, H], U32, name="w1_q", align_bytes=AL)
+        w1_sc = keep.tile([P, PASSES, H], U8, name="w1_sc", align_bytes=AL)
+        windows = []
+        for a in range(PASSES):
+            src = w1_raw[a][:].rearrange("p i (q t m) -> p t q m i", t=PACK, m=8)
+            for t in range(PACK):
+                nc.scalar.activation(
+                    w1_bf[:, a, t, :].rearrange("p (q m i) -> p q m i", m=8, i=PACK), src[:, t], ACT.Copy, scale=-1.0
+                )
+            if a == 0:
+                nc.scalar.dma_start(v_sc1[0:112, :], v_sc[4:116, :])
+            nc.vector.quantize_mx(
+                out=w1_q[:, a, :].bitcast(FP8X4),
+                scales=w1_sc[:, a, :],
+                in_=w1_bf[:, a].rearrange("p t c -> p (t c)"),
+            )
+            window = keep.tile([P, T2], F32, name="window%d" % a, tag="big%d" % a, align_bytes=AL)
+            nc.vector.memset(window[:], 0.0)
+            windows.append(window)
+
+        w4_q = keep.tile([P, PASSES, H // 2], I32, name="w4_q", align_bytes=AL)
+        w4_sc = keep.tile([P, PASSES, H // 4], I32, name="w4_sc", align_bytes=AL)
+        for a in range(PASSES):
+            nc.vector.tensor_copy(
+                w4_q[:, a, :].rearrange("p (t q w) -> p t q w", t=PACK, w=4),
+                w4_raw[:, a, :].rearrange("p (q t w) -> p t q w", t=PACK, w=4),
+            )
+            nc.vector.tensor_copy(
+                w4_sc[:, a, :].rearrange("p (t q w) -> p t q w", t=PACK, w=2),
+                w4_sc_raw[:, a, :].rearrange("p (q t w) -> p t q w", t=PACK, w=2),
+            )
+
+        v_q = [keep.tile([P, S], U32, name="v_q%d" % a, align_bytes=AL) for a in range(PASSES)]
+        nc.vector.tensor_copy(v_q[0][:], tab[0][:].bitcast(U32).indirect(idx[:]))
+        for half in range(S // HALF):
+            nc.vector.tensor_copy(
+                v_q[1][:, half * HALF : (half + 1) * HALF],
+                tab[1][:].bitcast(U32).indirect(idx[:, half * HALF // 16 : (half + 1) * HALF // 16]),
+            )
+        v_planes = [v_sc[:].bitcast(U8), v_sc1[:].bitcast(U8)]
+
+        w2_bf = keep.tile([P, N, PACK], BF16, name="w2_bf", align_bytes=AL)
+        w2_q = keep.tile([P, N], U32, name="w2_q", align_bytes=AL)
+        w2_sc = keep.tile([P, N], U8, name="w2_sc", align_bytes=AL)
+        nc.vector.tensor_copy(
+            w2_bf[:].rearrange("p (c i) t -> p c t i", i=4), w2_raw[:].rearrange("p t (c i) -> p c t i", i=4)
+        )
+        window = keep.tile([P, T2], F32, name="window3", tag="big3", align_bytes=AL)
+        nc.vector.memset(window[:], 0.0)
+        windows.append(window)
+        windows.append(windows[0])
+        nc.vector.quantize_mx(
+            out=w2_q[:].bitcast(FP8X4), scales=w2_sc[:], in_=w2_bf[:].rearrange("p n t -> p (n t)")
+        )
+
+        h_bf = keep.tile([P, S, PACK], BF16, name="h_bf", align_bytes=AL)
+        h_q = keep.tile([P, S], U32, name="h_q", align_bytes=AL)
+        h_sc = keep.tile([P, S], U8, name="h_sc", align_bytes=AL)
+
+        def features(c):
+            for j0 in range(c * CHUNK, (c + 1) * CHUNK, COLS):
+                cols = slice(j0, j0 + COLS)
+                diff = psum1.tile([P, PACK, COLS], F32, name="diff")
+                for t in range(PACK):
+                    rows = slice(t * COLS, (t + 1) * COLS)
+                    for a in range(PASSES):
+                        nc.tensor.matmul_mx(
+                            diff[:, t, :],
+                            lhsT=w1_q[:, a, rows].bitcast(FP8X4),
+                            lhsT_scale=w1_sc[:, a, rows],
+                            rhs=v_q[a][:, cols].bitcast(FP8X4),
+                            rhs_scale=v_planes[a][:, cols],
+                            start=(a == 0),
+                            stop=False,
+                        )
+                        nc.tensor.matmul_mx(
+                            diff[:, t, :],
+                            lhsT=w4_q[:, a, t * COLS // 2 : (t + 1) * COLS // 2].bitcast(U8).bitcast(FP4X4),
+                            lhsT_scale=w4_sc[:, a, t * COLS // 4 : (t + 1) * COLS // 4].bitcast(U8),
+                            rhs=v_q[a][:, cols].bitcast(FP8X4),
+                            rhs_scale=v_planes[a][:, cols],
+                            start=False,
+                            stop=(a == PASSES - 1),
+                        )
+                nc.scalar.activation(h_bf[:, cols, :], diff[:].rearrange("p t j -> p j t"), ACT.Square)
+
+        def quantise_h(c):
+            cols = slice(c * CHUNK, (c + 1) * CHUNK)
+            nc.vector.quantize_mx(
+                out=h_q[:, cols].bitcast(FP8X4),
+                scales=h_sc[:, cols],
+                in_=h_bf[:, cols, :].rearrange("p j t -> p (j t)"),
+            )
+
+        def pool(n, j0, width):
+            cols = slice(j0, j0 + width)
+            heads = slice(n * P, (n + 1) * P)
+            x = psum2.tile([P, width], F32, name="x", tag="x")
+            nc.tensor.matmul_mx(
+                x[:],
+                lhsT=w2_q[:, heads].bitcast(FP8X4),
+                lhsT_scale=w2_sc[:, heads],
+                rhs=h_q[:, cols].bitcast(FP8X4),
+                rhs_scale=h_sc[:, cols],
+                start=True,
+                stop=True,
+            )
+            y = ring.tile([P, width], F32, name="y", tag="y")
+            nc.scalar.activation(y[:], x[:], ACT.Sqrt, bias=ones[:])
+            z = ring.tile([P, width], F32, name="z", tag="z")
+            nc.vector.tensor_tensor(z[:], y[:], wgo_sb[:, cols], MULT)
+            return z
+
+        def place(n, j0, width, z):
+            nc.vector.tensor_copy(windows[n][:].indirect(idx2[:, j0 // 16 : (j0 + width) // 16]), z[:])
+            if j0 + width == S:
+                nc.sync.dma_start(out[n * P : (n + 1) * P, :], windows[n][:])
+
+        chunks = S // CHUNK
+        steps = [(n, c * CHUNK, CHUNK) for c in range(chunks) for n in range(2)]
+        steps += [(n, j0, HALF) for n in range(2, 4) for j0 in range(0, S, HALF)]
+        features(0)
+        features(1)
+        quantise_h(0)
+        pending = None
+        for n, j0, width in steps:
+            c = j0 // CHUNK
+            if n == 0 and c + 2 < chunks:
+                features(c + 2)
+            z = pool(n, j0, width)
+            if n == 1 and c + 1 < chunks:
+                quantise_h(c + 1)
+            if pending is not None:
+                place(*pending)
+            pending = (n, j0, width, z)
+        place(*pending)

@@ -33,76 +33,71 @@ def tile_list_replay_huber_novelty_kernel(
     with ExitStack() as ctx:
         lists = ctx.enter_context(tc.tile_pool(name="lists", bufs=1))
         keep = ctx.enter_context(tc.tile_pool(name="keep", bufs=1))
-        ring = ctx.enter_context(tc.tile_pool(name="ring", bufs=3))
-        psum1 = ctx.enter_context(tc.psum_pool(name="psum1", bufs=4))
-        psum2 = ctx.enter_context(tc.psum_pool(name="psum2", bufs=4))
+        ring = ctx.enter_context(tc.tile_pool(name="ring", bufs=6))
+        psum1 = ctx.enter_context(tc.psum_pool(name="psum1", bufs=6))
+        psum2 = ctx.enter_context(tc.psum_pool(name="psum2", bufs=2))
 
         idx = lists.tile([P, S // 16], U16, name="idx")
         idx2 = lists.tile([P, S // 16], U16, name="idx2")
 
-        tab_sc = keep.tile([P, T // 4], I32, name="tab_sc", align_bytes=AL)
+        tab_sc = keep.tile([P, T // 4], I32, name="tab_sc", tag="big1", align_bytes=AL)
         w4_sc_raw = keep.tile([P, PASSES, H // 4], I32, name="w4_sc_raw", align_bytes=AL)
-        v_sc1 = keep.tile([P, S // 4], I32, name="v_sc1", align_bytes=AL)
+        v_sc = keep.tile([P, PASSES, S // 4], I32, name="v_sc", align_bytes=AL)
         ones = keep.tile([P, 1], F32, name="ones")
         warm = keep.tile([P, 1], F32, name="warm")
         nc.vector.memset(w4_sc_raw[:], 0)
-        nc.vector.memset(tab_sc[:], 0)
-        nc.vector.memset(v_sc1[:], 0)
         nc.vector.memset(ones[:], 1.0)
-        nc.scalar.activation(warm[:], ones[:], ACT.Sqrt, bias=ones[:])
+        nc.gpsimd.memset(tab_sc[32:64, :], 0)
+        nc.gpsimd.memset(tab_sc[64:P, :], 0)
+        nc.gpsimd.memset(v_sc[:], 0)
+        windows = [keep.tile([P, T2], F32, name="window%d" % n, align_bytes=AL) for n in range(3)]
+        for window in windows:
+            for c0 in range(0, T2, HALF):
+                nc.gpsimd.memset(window[:, c0 : c0 + HALF], 0.0)
+        windows.append(windows[0])
 
         for q in range(4):
             nc.scalar.dma_start(
                 w4_sc_raw[32 * q : 32 * q + 4, :, :],
                 w4_scales[:, 4 * q : 4 * q + 4, :].rearrange("a r c -> r a c").bitcast(I32),
             )
-        nc.sync.dma_start(idx[:], offs)
-        w1_raw = []
-        for a in range(PASSES):
-            raw = keep.tile([P, PACK, H], F32, name="w1_raw%d" % a, tag="big%d" % a, align_bytes=AL)
+        nc.scalar.activation(warm[:], ones[:], ACT.Sqrt, bias=ones[:])
+
+        def load_w1(a):
+            raw = keep.tile([P, PACK, H], F32, name="w1_raw%d" % a, tag="w1_raw", align_bytes=AL)
             nc.sync.dma_start(raw[:], w1[a * K_PASS : (a + 1) * K_PASS, :].rearrange("(p i) c -> p i c", i=PACK))
-            w1_raw.append(raw)
+            return raw[:].rearrange("p i (q t m) -> p t q m i", t=PACK, m=8)
+
+        def load_table(a):
+            words = keep.tile([P, T], I32, name="tab%d" % a, tag="big%d" % a, align_bytes=AL)
+            nc.sync.dma_start(words[:], tab_words[a].rearrange("p t i -> p (t i)").bitcast(I32))
+            return words[:].bitcast(U32)
+
+        nc.sync.dma_start(tab_sc[0:32, :], tab_scales.rearrange("a q t -> q a t").bitcast(I32))
+        nc.sync.dma_start(idx[:], offs)
+        nc.sync.dma_start(idx2[:], offs2)
         w4_raw = keep.tile([P, PASSES, H // 2], I32, name="w4_raw", align_bytes=AL)
         nc.sync.dma_start(w4_raw[:], w4_words.rearrange("a p c -> p a c").bitcast(I32))
-        tab = []
-        for a in range(PASSES):
-            words = keep.tile([P, T], I32, name="tab%d" % a, tag="big%d" % (2 + a), align_bytes=AL)
-            nc.sync.dma_start(words[:], tab_words[a].rearrange("p t i -> p (t i)").bitcast(I32))
-            tab.append(words)
-        w2_raw = keep.tile([P, PACK, N], F32, name="w2_raw", align_bytes=AL)
-        w2_rows = w2.rearrange("(q t m) n -> t q m n", t=PACK, m=8)
-        for t in range(PACK):
-            nc.sync.dma_start(w2_raw[:, t, :], w2_rows[t])
-        wgo_sb = keep.tile([P, S], F32, name="wgo_sb", align_bytes=AL)
-        nc.sync.dma_start(wgo_sb[:], wgo)
-        nc.sync.dma_start(idx2[:], offs2)
+        w1_first = load_w1(0)
+        tab_first = load_table(0)
 
+        picked_sc = keep.tile([P, S // 4], I32, name="picked_sc", align_bytes=AL)
+        nc.vector.tensor_copy(picked_sc[:].bitcast(U8), tab_sc[:].bitcast(U8).indirect(idx[:]))
+        tab_second = load_table(1)
         for q in range(4):
-            nc.gpsimd.dma_start(tab_sc[32 * q : 32 * q + 8, :], tab_scales[:, 4 * q : 4 * q + 4, :].bitcast(I32))
-
-        v_sc = keep.tile([P, S // 4], I32, name="v_sc", align_bytes=AL)
-        nc.vector.tensor_copy(v_sc[:].bitcast(U8), tab_sc[:].bitcast(U8).indirect(idx[:]))
+            nc.sync.dma_start(v_sc[32 * q : 32 * q + 4, :, :], picked_sc[8 * q : 8 * q + 8, :])
 
         w1_bf = keep.tile([P, PASSES, PACK, COLS * PACK], BF16, name="w1_bf", align_bytes=AL)
         w1_q = keep.tile([P, PASSES, H], U32, name="w1_q", align_bytes=AL)
         w1_sc = keep.tile([P, PASSES, H], U8, name="w1_sc", align_bytes=AL)
-        windows = []
-        for a in range(PASSES):
-            src = w1_raw[a][:].rearrange("p i (q t m) -> p t q m i", t=PACK, m=8)
-            for t in range(PACK):
-                nc.scalar.activation(
-                    w1_bf[:, a, t, :].rearrange("p (q m i) -> p q m i", m=8, i=PACK), src[:, t], ACT.Copy, scale=-1.0
-                )
-            if a == 0:
-                nc.scalar.dma_start(v_sc1[0:112, :], v_sc[4:116, :])
-            nc.vector.quantize_mx(
-                out=w1_q[:, a, :].bitcast(FP8X4),
-                scales=w1_sc[:, a, :],
-                in_=w1_bf[:, a].rearrange("p t c -> p (t c)"),
-            )
-            window = keep.tile([P, T2], F32, name="window%d" % a, tag="big%d" % a, align_bytes=AL)
-            nc.vector.memset(window[:], 0.0)
-            windows.append(window)
+
+        def grouped(a, t):
+            return w1_bf[:, a, t, :].rearrange("p (q m i) -> p q m i", m=8, i=PACK)
+
+        for t in range(PACK):
+            nc.scalar.activation(grouped(0, t), w1_first[:, t], ACT.Copy, scale=-1.0)
+        w1_second = load_w1(1)
+        v_planes = [v_sc[:, a, :].bitcast(U8) for a in range(PASSES)]
 
         w4_q = keep.tile([P, PASSES, H // 2], I32, name="w4_q", align_bytes=AL)
         w4_sc = keep.tile([P, PASSES, H // 4], I32, name="w4_sc", align_bytes=AL)
@@ -115,67 +110,93 @@ def tile_list_replay_huber_novelty_kernel(
                 w4_sc[:, a, :].rearrange("p (t q w) -> p t q w", t=PACK, w=2),
                 w4_sc_raw[:, a, :].rearrange("p (q t w) -> p t q w", t=PACK, w=2),
             )
+        nc.vector.quantize_mx(
+            out=w1_q[:, 0, :].bitcast(FP8X4), scales=w1_sc[:, 0, :], in_=w1_bf[:, 0].rearrange("p t c -> p (t c)")
+        )
 
         v_q = [keep.tile([P, S], U32, name="v_q%d" % a, align_bytes=AL) for a in range(PASSES)]
-        nc.vector.tensor_copy(v_q[0][:], tab[0][:].bitcast(U32).indirect(idx[:]))
+        nc.vector.tensor_copy(v_q[0][:], tab_first.indirect(idx[:]))
+        w2_raw = keep.tile([P, PACK, N], F32, name="w2_raw", tag="big0", align_bytes=AL)
+        w2_rows = w2.rearrange("(q t m) n -> t q m n", t=PACK, m=8)
+        for t in range(PACK):
+            nc.sync.dma_start(w2_raw[:, t, :], w2_rows[t])
         for half in range(S // HALF):
             nc.vector.tensor_copy(
                 v_q[1][:, half * HALF : (half + 1) * HALF],
-                tab[1][:].bitcast(U32).indirect(idx[:, half * HALF // 16 : (half + 1) * HALF // 16]),
+                tab_second.indirect(idx[:, half * HALF // 16 : (half + 1) * HALF // 16]),
             )
-        v_planes = [v_sc[:].bitcast(U8), v_sc1[:].bitcast(U8)]
+        wgo_sb = keep.tile([P, S], F32, name="wgo_sb", tag="big1", align_bytes=AL)
+        nc.sync.dma_start(wgo_sb[:], wgo)
 
-        w2_bf = keep.tile([P, N, PACK], BF16, name="w2_bf", align_bytes=AL)
+        for t in range(PACK):
+            if t % 2 == 0:
+                nc.vector.tensor_scalar(grouped(1, t), w1_second[:, t], -1.0, None, MULT)
+            else:
+                nc.scalar.activation(grouped(1, t), w1_second[:, t], ACT.Copy, scale=-1.0)
+        for t in range(PACK):
+            rows = slice(t * COLS, (t + 1) * COLS)
+            nc.vector.quantize_mx(out=w1_q[:, 1, rows].bitcast(FP8X4), scales=w1_sc[:, 1, rows], in_=w1_bf[:, 1, t, :])
+
         w2_q = keep.tile([P, N], U32, name="w2_q", align_bytes=AL)
         w2_sc = keep.tile([P, N], U8, name="w2_sc", align_bytes=AL)
-        nc.vector.tensor_copy(
-            w2_bf[:].rearrange("p (c i) t -> p c t i", i=4), w2_raw[:].rearrange("p t (c i) -> p c t i", i=4)
-        )
-        window = keep.tile([P, T2], F32, name="window3", tag="big3", align_bytes=AL)
-        nc.vector.memset(window[:], 0.0)
-        windows.append(window)
-        windows.append(windows[0])
-        nc.vector.quantize_mx(
-            out=w2_q[:].bitcast(FP8X4), scales=w2_sc[:], in_=w2_bf[:].rearrange("p n t -> p (n t)")
-        )
 
-        h_bf = keep.tile([P, S, PACK], BF16, name="h_bf", align_bytes=AL)
+        def quantise_w2(heads, rounded):
+            nc.vector.quantize_mx(
+                out=w2_q[:, heads].bitcast(FP8X4), scales=w2_sc[:, heads], in_=rounded[:].rearrange("p n t -> p (n t)")
+            )
+
+        w2_low = keep.tile([P, N // 2, PACK], BF16, name="w2_low", align_bytes=AL)
+        nc.vector.tensor_copy(
+            w2_low[:].rearrange("p (c i) t -> p c t i", i=4),
+            w2_raw[:, :, 0 : N // 2].rearrange("p t (c i) -> p c t i", i=4),
+        )
+        quantise_w2(slice(0, N // 2), w2_low)
+
+        h_bf = [
+            keep.tile([P, CHUNK, PACK], BF16, name="h_bf%d" % c, tag="h_bf%d" % c, align_bytes=AL)
+            for c in range(S // CHUNK)
+        ]
         h_q = keep.tile([P, S], U32, name="h_q", align_bytes=AL)
         h_sc = keep.tile([P, S], U8, name="h_sc", align_bytes=AL)
 
-        def features(c):
-            for j0 in range(c * CHUNK, (c + 1) * CHUNK, COLS):
-                cols = slice(j0, j0 + COLS)
-                diff = psum1.tile([P, PACK, COLS], F32, name="diff")
-                for t in range(PACK):
-                    rows = slice(t * COLS, (t + 1) * COLS)
-                    for a in range(PASSES):
-                        nc.tensor.matmul_mx(
-                            diff[:, t, :],
-                            lhsT=w1_q[:, a, rows].bitcast(FP8X4),
-                            lhsT_scale=w1_sc[:, a, rows],
-                            rhs=v_q[a][:, cols].bitcast(FP8X4),
-                            rhs_scale=v_planes[a][:, cols],
-                            start=(a == 0),
-                            stop=False,
-                        )
-                        nc.tensor.matmul_mx(
-                            diff[:, t, :],
-                            lhsT=w4_q[:, a, t * COLS // 2 : (t + 1) * COLS // 2].bitcast(U8).bitcast(FP4X4),
-                            lhsT_scale=w4_sc[:, a, t * COLS // 4 : (t + 1) * COLS // 4].bitcast(U8),
-                            rhs=v_q[a][:, cols].bitcast(FP8X4),
-                            rhs_scale=v_planes[a][:, cols],
-                            start=False,
-                            stop=(a == PASSES - 1),
-                        )
-                nc.scalar.activation(h_bf[:, cols, :], diff[:].rearrange("p t j -> p j t"), ACT.Square)
+        def one_pass(diff, j0, t, step):
+            cols = slice(j0, j0 + COLS)
+            online, a = ((True, 0), (False, 0), (False, 1), (True, 1))[step]
+            if online:
+                rows = slice(t * COLS, (t + 1) * COLS)
+                codes, scales = w1_q[:, a, rows].bitcast(FP8X4), w1_sc[:, a, rows]
+            else:
+                codes = w4_q[:, a, t * COLS // 2 : (t + 1) * COLS // 2].bitcast(U8).bitcast(FP4X4)
+                scales = w4_sc[:, a, t * COLS // 4 : (t + 1) * COLS // 4].bitcast(U8)
+            nc.tensor.matmul_mx(
+                diff[:, t, :],
+                lhsT=codes,
+                lhsT_scale=scales,
+                rhs=v_q[a][:, cols].bitcast(FP8X4),
+                rhs_scale=v_planes[a][:, cols],
+                start=(step == 0),
+                stop=(step == 3),
+            )
+
+        early = {}
+        for j0 in range(0, 6 * COLS, COLS):
+            early[j0] = psum1.tile([P, PACK, COLS], F32, name="diff", tag="diff")
+            for step in range(3):
+                one_pass(early[j0], j0, 0, step)
+
+        def features(j0):
+            diff = early[j0] if j0 in early else psum1.tile([P, PACK, COLS], F32, name="diff", tag="diff")
+            for t in range(PACK):
+                for step in range(3 if (j0 in early and t == 0) else 0, 4):
+                    one_pass(diff, j0, t, step)
+            nc.scalar.activation(h_bf[j0 // CHUNK][:, j0 % CHUNK : j0 % CHUNK + COLS, :], diff[:].rearrange("p t j -> p j t"), ACT.Square)
 
         def quantise_h(c):
             cols = slice(c * CHUNK, (c + 1) * CHUNK)
             nc.vector.quantize_mx(
                 out=h_q[:, cols].bitcast(FP8X4),
                 scales=h_sc[:, cols],
-                in_=h_bf[:, cols, :].rearrange("p j t -> p (j t)"),
+                in_=h_bf[c][:].rearrange("p j t -> p (j t)"),
             )
 
         def pool(n, j0, width):
@@ -193,30 +214,37 @@ def tile_list_replay_huber_novelty_kernel(
             )
             y = ring.tile([P, width], F32, name="y", tag="y")
             nc.scalar.activation(y[:], x[:], ACT.Sqrt, bias=ones[:])
-            z = ring.tile([P, width], F32, name="z", tag="z")
-            nc.vector.tensor_tensor(z[:], y[:], wgo_sb[:, cols], MULT)
-            return z
+            return y
 
         def place(n, j0, width, z):
-            nc.vector.tensor_copy(windows[n][:].indirect(idx2[:, j0 // 16 : (j0 + width) // 16]), z[:])
+            nc.vector.tensor_tensor(
+                windows[n][:].indirect(idx2[:, j0 // 16 : (j0 + width) // 16]), z[:], wgo_sb[:, j0 : j0 + width], MULT
+            )
             if j0 + width == S:
                 nc.sync.dma_start(out[n * P : (n + 1) * P, :], windows[n][:])
 
-        chunks = S // CHUNK
-        steps = [(n, c * CHUNK, CHUNK) for c in range(chunks) for n in range(2)]
-        steps += [(n, j0, HALF) for n in range(2, 4) for j0 in range(0, S, HALF)]
         features(0)
-        features(1)
+        features(COLS)
         quantise_h(0)
-        pending = None
-        for n, j0, width in steps:
-            c = j0 // CHUNK
-            if n == 0 and c + 2 < chunks:
-                features(c + 2)
-            z = pool(n, j0, width)
-            if n == 1 and c + 1 < chunks:
-                quantise_h(c + 1)
-            if pending is not None:
-                place(*pending)
-            pending = (n, j0, width, z)
-        place(*pending)
+        for j0 in range(0, S, CHUNK):
+            ahead = j0 + CHUNK
+            first = pool(0, j0, CHUNK)
+            if ahead < S:
+                features(ahead)
+                features(ahead + COLS)
+            second = pool(1, j0, CHUNK)
+            place(0, j0, CHUNK, first)
+            if ahead < S:
+                quantise_h(ahead // CHUNK)
+            place(1, j0, CHUNK, second)
+        w2_high = keep.tile([P, N // 2, PACK], BF16, name="w2_high", tag="h_bf0", align_bytes=AL)
+        for n in range(2):
+            nc.scalar.activation(
+                w2_high[:, n * P : (n + 1) * P, :],
+                w2_raw[:, :, (n + 2) * P : (n + 3) * P].rearrange("p t n -> p n t"),
+                ACT.Copy,
+            )
+        quantise_w2(slice(N // 2, N), w2_high)
+        for n in range(2, 4):
+            for j0 in range(0, S, HALF):
+                place(n, j0, HALF, pool(n, j0, HALF))

@@ -18,12 +18,20 @@ MULT = mybir.AluOpType.mult
 
 P = 128
 PACK = 4
+RUN = 8
+QUADS = 4
 K_PASS = P * PACK
 PASSES = K // K_PASS
+LIST_ROWS = 16
 COLS = 128
 CHUNK = 256
 HALF = 512
-AL = 64
+DIFF_BANKS = 6
+EARLY_TILES = 3
+SCORE_BUFS = 2 * EARLY_TILES
+ALIGN = 64
+
+GROUP = ((True, 0), (False, 0), (False, 1), (True, 1))
 
 
 def tile_list_replay_huber_novelty_kernel(
@@ -33,99 +41,107 @@ def tile_list_replay_huber_novelty_kernel(
     with ExitStack() as ctx:
         lists = ctx.enter_context(tc.tile_pool(name="lists", bufs=1))
         keep = ctx.enter_context(tc.tile_pool(name="keep", bufs=1))
-        ring = ctx.enter_context(tc.tile_pool(name="ring", bufs=6))
-        psum1 = ctx.enter_context(tc.psum_pool(name="psum1", bufs=6))
-        psum2 = ctx.enter_context(tc.psum_pool(name="psum2", bufs=2))
+        ring = ctx.enter_context(tc.tile_pool(name="ring", bufs=SCORE_BUFS))
+        diff_banks = ctx.enter_context(tc.psum_pool(name="diff_banks", bufs=DIFF_BANKS))
+        sum_banks = ctx.enter_context(tc.psum_pool(name="sum_banks", bufs=8 - DIFF_BANKS))
 
-        idx = lists.tile([P, S // 16], U16, name="idx")
-        idx2 = lists.tile([P, S // 16], U16, name="idx2")
+        idx = lists.tile([P, S // LIST_ROWS], U16, name="idx")
+        idx2 = lists.tile([P, S // LIST_ROWS], U16, name="idx2")
 
-        tab_sc = keep.tile([P, T // 4], I32, name="tab_sc", tag="big1", align_bytes=AL)
-        w4_sc_raw = keep.tile([P, PASSES, H // 4], I32, name="w4_sc_raw", align_bytes=AL)
-        v_sc = keep.tile([P, PASSES, S // 4], I32, name="v_sc", align_bytes=AL)
-        ones = keep.tile([P, 1], F32, name="ones")
-        warm = keep.tile([P, 1], F32, name="warm")
+        tab_sc = keep.tile([P, T // 4], I32, name="tab_sc", tag="second_table", align_bytes=ALIGN)
+        w4_sc_raw = keep.tile([P, PASSES, H // 4], I32, name="w4_sc_raw", align_bytes=ALIGN)
+        v_sc = keep.tile([P, PASSES, S // 4], I32, name="v_sc", align_bytes=ALIGN)
+        seed = keep.tile([P, 1], F32, name="seed")
+        one = keep.tile([P, 1], F32, name="one")
         nc.vector.memset(w4_sc_raw[:], 0)
-        nc.vector.memset(ones[:], 1.0)
-        nc.gpsimd.memset(tab_sc[32:64, :], 0)
-        nc.gpsimd.memset(tab_sc[64:P, :], 0)
-        nc.gpsimd.memset(v_sc[:], 0)
-        windows = [keep.tile([P, T2], F32, name="window%d" % n, align_bytes=AL) for n in range(3)]
-        for window in windows:
-            for c0 in range(0, T2, HALF):
-                nc.gpsimd.memset(window[:, c0 : c0 + HALF], 0.0)
-        windows.append(windows[0])
+        nc.vector.memset(seed[:], 1.0)
+        nc.vector.memset(tab_sc[32:64, :], 0)
+        nc.vector.memset(tab_sc[64:P, :], 0)
+        nc.vector.memset(v_sc[:], 0)
 
-        for q in range(4):
+        windows = []
+
+        def new_window(tag, engine, piece):
+            window = keep.tile([P, T2], F32, name="window%d" % len(windows), tag=tag, align_bytes=ALIGN)
+            for c0 in range(0, T2, piece):
+                engine.memset(window[:, c0 : c0 + piece], 0.0)
+            windows.append(window)
+
+        new_window("window0", nc.vector, T2)
+
+        for quad in range(QUADS):
             nc.scalar.dma_start(
-                w4_sc_raw[32 * q : 32 * q + 4, :, :],
-                w4_scales[:, 4 * q : 4 * q + 4, :].rearrange("a r c -> r a c").bitcast(I32),
+                w4_sc_raw[32 * quad : 32 * quad + 4, :, :],
+                w4_scales[:, 4 * quad : 4 * quad + 4, :].rearrange("a r c -> r a c").bitcast(I32),
             )
-        nc.scalar.activation(warm[:], ones[:], ACT.Sqrt, bias=ones[:])
+        nc.scalar.activation(one[:], seed[:], ACT.Sqrt)
 
         def load_w1(a):
-            raw = keep.tile([P, PACK, H], F32, name="w1_raw%d" % a, tag="w1_raw", align_bytes=AL)
+            raw = keep.tile([P, PACK, H], F32, name="w1_raw%d" % a, tag="w1_raw", align_bytes=ALIGN)
             nc.sync.dma_start(raw[:], w1[a * K_PASS : (a + 1) * K_PASS, :].rearrange("(p i) c -> p i c", i=PACK))
-            return raw[:].rearrange("p i (q t m) -> p t q m i", t=PACK, m=8)
+            return raw[:].rearrange("p i (q t m) -> p t q m i", t=PACK, m=RUN)
 
-        def load_table(a):
-            words = keep.tile([P, T], I32, name="tab%d" % a, tag="big%d" % a, align_bytes=AL)
+        def load_table(a, tag):
+            words = keep.tile([P, T], I32, name="tab%d" % a, tag=tag, align_bytes=ALIGN)
             nc.sync.dma_start(words[:], tab_words[a].rearrange("p t i -> p (t i)").bitcast(I32))
             return words[:].bitcast(U32)
 
         nc.sync.dma_start(tab_sc[0:32, :], tab_scales.rearrange("a q t -> q a t").bitcast(I32))
         nc.sync.dma_start(idx[:], offs)
         nc.sync.dma_start(idx2[:], offs2)
-        w4_raw = keep.tile([P, PASSES, H // 2], I32, name="w4_raw", align_bytes=AL)
+        w4_raw = keep.tile([P, PASSES, H // 2], I32, name="w4_raw", tag="window1", align_bytes=ALIGN)
         nc.sync.dma_start(w4_raw[:], w4_words.rearrange("a p c -> p a c").bitcast(I32))
         w1_first = load_w1(0)
-        tab_first = load_table(0)
+        tab_first = load_table(0, "first_table")
 
-        picked_sc = keep.tile([P, S // 4], I32, name="picked_sc", align_bytes=AL)
+        picked_sc = keep.tile([P, S // 4], I32, name="picked_sc", align_bytes=ALIGN)
         nc.vector.tensor_copy(picked_sc[:].bitcast(U8), tab_sc[:].bitcast(U8).indirect(idx[:]))
-        tab_second = load_table(1)
-        for q in range(4):
-            nc.sync.dma_start(v_sc[32 * q : 32 * q + 4, :, :], picked_sc[8 * q : 8 * q + 8, :])
+        tab_second = load_table(1, "second_table")
+        for quad in range(QUADS):
+            nc.sync.dma_start(v_sc[32 * quad : 32 * quad + 4, :, :], picked_sc[8 * quad : 8 * quad + 8, :])
 
-        w1_bf = keep.tile([P, PASSES, PACK, COLS * PACK], BF16, name="w1_bf", align_bytes=AL)
-        w1_q = keep.tile([P, PASSES, H], U32, name="w1_q", align_bytes=AL)
-        w1_sc = keep.tile([P, PASSES, H], U8, name="w1_sc", align_bytes=AL)
+        w1_bf = [
+            keep.tile([P, PACK, P * PACK], BF16, name="w1_bf%d" % a, tag="w1_bf%d" % a, align_bytes=ALIGN)
+            for a in range(PASSES)
+        ]
+        w1_q = keep.tile([P, PASSES, H], U32, name="w1_q", align_bytes=ALIGN)
+        w1_sc = keep.tile([P, PASSES, H], U8, name="w1_sc", align_bytes=ALIGN)
 
         def grouped(a, t):
-            return w1_bf[:, a, t, :].rearrange("p (q m i) -> p q m i", m=8, i=PACK)
+            return w1_bf[a][:, t, :].rearrange("p (q m i) -> p q m i", m=RUN, i=PACK)
 
         for t in range(PACK):
             nc.scalar.activation(grouped(0, t), w1_first[:, t], ACT.Copy, scale=-1.0)
         w1_second = load_w1(1)
-        v_planes = [v_sc[:, a, :].bitcast(U8) for a in range(PASSES)]
 
-        w4_q = keep.tile([P, PASSES, H // 2], I32, name="w4_q", align_bytes=AL)
-        w4_sc = keep.tile([P, PASSES, H // 4], I32, name="w4_sc", align_bytes=AL)
+        w4_q = keep.tile([P, PASSES, H // 2], I32, name="w4_q", align_bytes=ALIGN)
+        w4_sc = keep.tile([P, PASSES, H // 4], I32, name="w4_sc", align_bytes=ALIGN)
         for a in range(PASSES):
             nc.vector.tensor_copy(
-                w4_q[:, a, :].rearrange("p (t q w) -> p t q w", t=PACK, w=4),
-                w4_raw[:, a, :].rearrange("p (q t w) -> p t q w", t=PACK, w=4),
+                w4_q[:, a, :].rearrange("p (t q w) -> p t q w", t=PACK, w=RUN // 2),
+                w4_raw[:, a, :].rearrange("p (q t w) -> p t q w", t=PACK, w=RUN // 2),
             )
             nc.vector.tensor_copy(
-                w4_sc[:, a, :].rearrange("p (t q w) -> p t q w", t=PACK, w=2),
-                w4_sc_raw[:, a, :].rearrange("p (q t w) -> p t q w", t=PACK, w=2),
+                w4_sc[:, a, :].rearrange("p (t q w) -> p t q w", t=PACK, w=RUN // 4),
+                w4_sc_raw[:, a, :].rearrange("p (q t w) -> p t q w", t=PACK, w=RUN // 4),
             )
         nc.vector.quantize_mx(
-            out=w1_q[:, 0, :].bitcast(FP8X4), scales=w1_sc[:, 0, :], in_=w1_bf[:, 0].rearrange("p t c -> p (t c)")
+            out=w1_q[:, 0, :].bitcast(FP8X4), scales=w1_sc[:, 0, :], in_=w1_bf[0][:].rearrange("p t c -> p (t c)")
         )
+        new_window("window1", nc.gpsimd, CHUNK)
+        new_window("w1_bf0", nc.vector, T2)
 
-        v_q = [keep.tile([P, S], U32, name="v_q%d" % a, align_bytes=AL) for a in range(PASSES)]
+        v_q = [keep.tile([P, S], U32, name="v_q%d" % a, align_bytes=ALIGN) for a in range(PASSES)]
         nc.vector.tensor_copy(v_q[0][:], tab_first.indirect(idx[:]))
-        w2_raw = keep.tile([P, PACK, N], F32, name="w2_raw", tag="big0", align_bytes=AL)
-        w2_rows = w2.rearrange("(q t m) n -> t q m n", t=PACK, m=8)
+        w2_raw = keep.tile([P, PACK, N], F32, name="w2_raw", tag="first_table", align_bytes=ALIGN)
+        w2_rows = w2.rearrange("(q t m) n -> t q m n", t=PACK, m=RUN)
         for t in range(PACK):
             nc.sync.dma_start(w2_raw[:, t, :], w2_rows[t])
-        for half in range(S // HALF):
+        for j0 in range(0, S, HALF):
             nc.vector.tensor_copy(
-                v_q[1][:, half * HALF : (half + 1) * HALF],
-                tab_second.indirect(idx[:, half * HALF // 16 : (half + 1) * HALF // 16]),
+                v_q[1][:, j0 : j0 + HALF], tab_second.indirect(idx[:, j0 // LIST_ROWS : (j0 + HALF) // LIST_ROWS])
             )
-        wgo_sb = keep.tile([P, S], F32, name="wgo_sb", tag="big1", align_bytes=AL)
+        wgo_sb = keep.tile([P, S], F32, name="wgo_sb", tag="second_table", align_bytes=ALIGN)
         nc.sync.dma_start(wgo_sb[:], wgo)
 
         for t in range(PACK):
@@ -134,75 +150,81 @@ def tile_list_replay_huber_novelty_kernel(
             else:
                 nc.scalar.activation(grouped(1, t), w1_second[:, t], ACT.Copy, scale=-1.0)
         for t in range(PACK):
-            rows = slice(t * COLS, (t + 1) * COLS)
-            nc.vector.quantize_mx(out=w1_q[:, 1, rows].bitcast(FP8X4), scales=w1_sc[:, 1, rows], in_=w1_bf[:, 1, t, :])
+            features = slice(t * P, (t + 1) * P)
+            nc.vector.quantize_mx(
+                out=w1_q[:, 1, features].bitcast(FP8X4), scales=w1_sc[:, 1, features], in_=w1_bf[1][:, t, :]
+            )
 
-        w2_q = keep.tile([P, N], U32, name="w2_q", align_bytes=AL)
-        w2_sc = keep.tile([P, N], U8, name="w2_sc", align_bytes=AL)
+        w2_q = keep.tile([P, N], U32, name="w2_q", align_bytes=ALIGN)
+        w2_sc = keep.tile([P, N], U8, name="w2_sc", align_bytes=ALIGN)
 
         def quantise_w2(heads, rounded):
             nc.vector.quantize_mx(
                 out=w2_q[:, heads].bitcast(FP8X4), scales=w2_sc[:, heads], in_=rounded[:].rearrange("p n t -> p (n t)")
             )
 
-        w2_low = keep.tile([P, N // 2, PACK], BF16, name="w2_low", align_bytes=AL)
-        nc.vector.tensor_copy(
-            w2_low[:].rearrange("p (c i) t -> p c t i", i=4),
-            w2_raw[:, :, 0 : N // 2].rearrange("p t (c i) -> p c t i", i=4),
-        )
-        quantise_w2(slice(0, N // 2), w2_low)
+        for first, last in ((0, 2 * P), (2 * P, EARLY_TILES * P)):
+            rounded = keep.tile([P, last - first, PACK], BF16, name="w2_bf%d" % first, align_bytes=ALIGN)
+            nc.vector.tensor_copy(
+                rounded[:].rearrange("p (c i) t -> p c t i", i=4),
+                w2_raw[:, :, first:last].rearrange("p t (c i) -> p c t i", i=4),
+            )
+            quantise_w2(slice(first, last), rounded)
 
         h_bf = [
-            keep.tile([P, CHUNK, PACK], BF16, name="h_bf%d" % c, tag="h_bf%d" % c, align_bytes=AL)
+            keep.tile([P, CHUNK, PACK], BF16, name="h_bf%d" % c, tag="h_bf%d" % c, align_bytes=ALIGN)
             for c in range(S // CHUNK)
         ]
-        h_q = keep.tile([P, S], U32, name="h_q", align_bytes=AL)
-        h_sc = keep.tile([P, S], U8, name="h_sc", align_bytes=AL)
+        h_q = keep.tile([P, S], U32, name="h_q", align_bytes=ALIGN)
+        h_sc = keep.tile([P, S], U8, name="h_sc", align_bytes=ALIGN)
 
         def one_pass(diff, j0, t, step):
             cols = slice(j0, j0 + COLS)
-            online, a = ((True, 0), (False, 0), (False, 1), (True, 1))[step]
+            online, a = GROUP[step]
             if online:
-                rows = slice(t * COLS, (t + 1) * COLS)
-                codes, scales = w1_q[:, a, rows].bitcast(FP8X4), w1_sc[:, a, rows]
+                codes = w1_q[:, a, t * P : (t + 1) * P].bitcast(FP8X4)
+                scales = w1_sc[:, a, t * P : (t + 1) * P]
             else:
-                codes = w4_q[:, a, t * COLS // 2 : (t + 1) * COLS // 2].bitcast(U8).bitcast(FP4X4)
-                scales = w4_sc[:, a, t * COLS // 4 : (t + 1) * COLS // 4].bitcast(U8)
+                codes = w4_q[:, a, t * P // 2 : (t + 1) * P // 2].bitcast(U8).bitcast(FP4X4)
+                scales = w4_sc[:, a, t * P // 4 : (t + 1) * P // 4].bitcast(U8)
             nc.tensor.matmul_mx(
                 diff[:, t, :],
                 lhsT=codes,
                 lhsT_scale=scales,
                 rhs=v_q[a][:, cols].bitcast(FP8X4),
-                rhs_scale=v_planes[a][:, cols],
+                rhs_scale=v_sc[:, a, :].bitcast(U8)[:, cols],
                 start=(step == 0),
-                stop=(step == 3),
+                stop=(step == len(GROUP) - 1),
             )
 
-        early = {}
-        for j0 in range(0, 6 * COLS, COLS):
-            early[j0] = psum1.tile([P, PACK, COLS], F32, name="diff", tag="diff")
-            for step in range(3):
-                one_pass(early[j0], j0, 0, step)
+        opened = {}
+        for j0 in range(0, DIFF_BANKS * COLS, COLS):
+            opened[j0] = diff_banks.tile([P, PACK, COLS], F32, name="diff", tag="diff")
+            for step in range(len(GROUP) - 1):
+                one_pass(opened[j0], j0, 0, step)
 
-        def features(j0):
-            diff = early[j0] if j0 in early else psum1.tile([P, PACK, COLS], F32, name="diff", tag="diff")
+        def square_differences(j0):
+            diff = opened[j0] if j0 in opened else diff_banks.tile([P, PACK, COLS], F32, name="diff", tag="diff")
             for t in range(PACK):
-                for step in range(3 if (j0 in early and t == 0) else 0, 4):
+                done = len(GROUP) - 1 if (j0 in opened and t == 0) else 0
+                for step in range(done, len(GROUP)):
                     one_pass(diff, j0, t, step)
-            nc.scalar.activation(h_bf[j0 // CHUNK][:, j0 % CHUNK : j0 % CHUNK + COLS, :], diff[:].rearrange("p t j -> p j t"), ACT.Square)
+            nc.scalar.activation(
+                h_bf[j0 // CHUNK][:, j0 % CHUNK : j0 % CHUNK + COLS, :], diff[:].rearrange("p t j -> p j t"), ACT.Square
+            )
 
-        def quantise_h(c):
-            cols = slice(c * CHUNK, (c + 1) * CHUNK)
+        def quantise_h(j0):
+            cols = slice(j0, j0 + CHUNK)
             nc.vector.quantize_mx(
                 out=h_q[:, cols].bitcast(FP8X4),
                 scales=h_sc[:, cols],
-                in_=h_bf[c][:].rearrange("p j t -> p (j t)"),
+                in_=h_bf[j0 // CHUNK][:].rearrange("p j t -> p (j t)"),
             )
 
-        def pool(n, j0, width):
+        def score(n, j0, width):
             cols = slice(j0, j0 + width)
             heads = slice(n * P, (n + 1) * P)
-            x = psum2.tile([P, width], F32, name="x", tag="x")
+            x = sum_banks.tile([P, width], F32, name="x", tag="x")
             nc.tensor.matmul_mx(
                 x[:],
                 lhsT=w2_q[:, heads].bitcast(FP8X4),
@@ -213,38 +235,35 @@ def tile_list_replay_huber_novelty_kernel(
                 stop=True,
             )
             y = ring.tile([P, width], F32, name="y", tag="y")
-            nc.scalar.activation(y[:], x[:], ACT.Sqrt, bias=ones[:])
+            nc.scalar.activation(y[:], x[:], ACT.Sqrt, bias=one[:])
             return y
 
-        def place(n, j0, width, z):
-            nc.vector.tensor_tensor(
-                windows[n][:].indirect(idx2[:, j0 // 16 : (j0 + width) // 16]), z[:], wgo_sb[:, j0 : j0 + width], MULT
-            )
+        def place(n, j0, width, y):
+            places = idx2[:, j0 // LIST_ROWS : (j0 + width) // LIST_ROWS]
+            nc.vector.tensor_tensor(windows[n][:].indirect(places), y[:], wgo_sb[:, j0 : j0 + width], MULT)
             if j0 + width == S:
                 nc.sync.dma_start(out[n * P : (n + 1) * P, :], windows[n][:])
 
-        features(0)
-        features(COLS)
+        square_differences(0)
+        square_differences(COLS)
         quantise_h(0)
         for j0 in range(0, S, CHUNK):
             ahead = j0 + CHUNK
-            first = pool(0, j0, CHUNK)
+            scores = [score(0, j0, CHUNK)]
             if ahead < S:
-                features(ahead)
-                features(ahead + COLS)
-            second = pool(1, j0, CHUNK)
-            place(0, j0, CHUNK, first)
+                square_differences(ahead)
+                square_differences(ahead + COLS)
+            scores += [score(n, j0, CHUNK) for n in range(1, EARLY_TILES)]
+            place(0, j0, CHUNK, scores[0])
             if ahead < S:
-                quantise_h(ahead // CHUNK)
-            place(1, j0, CHUNK, second)
-        w2_high = keep.tile([P, N // 2, PACK], BF16, name="w2_high", tag="h_bf0", align_bytes=AL)
-        for n in range(2):
-            nc.scalar.activation(
-                w2_high[:, n * P : (n + 1) * P, :],
-                w2_raw[:, :, (n + 2) * P : (n + 3) * P].rearrange("p t n -> p n t"),
-                ACT.Copy,
-            )
-        quantise_w2(slice(N // 2, N), w2_high)
-        for n in range(2, 4):
-            for j0 in range(0, S, HALF):
-                place(n, j0, HALF, pool(n, j0, HALF))
+                quantise_h(ahead)
+            for n in range(1, EARLY_TILES):
+                place(n, j0, CHUNK, scores[n])
+
+        heads = slice(EARLY_TILES * P, N)
+        rounded = keep.tile([P, P, PACK], BF16, name="w2_last", tag="h_bf1", align_bytes=ALIGN)
+        nc.scalar.activation(rounded[:], w2_raw[:, :, heads].rearrange("p t n -> p n t"), ACT.Copy)
+        quantise_w2(heads, rounded)
+        new_window("first_table", nc.gpsimd, CHUNK)
+        for j0 in range(0, S, HALF):
+            place(EARLY_TILES, j0, HALF, score(EARLY_TILES, j0, HALF))

@@ -26,12 +26,11 @@ LIST_ROWS = 16
 COLS = 128
 CHUNK = 256
 HALF = 512
-DIFF_BANKS = 6
-EARLY_TILES = 3
-SCORE_BUFS = 2 * EARLY_TILES
+AHEAD = (3, 2, 2, 0)
+EARLY_TILES = 2
 ALIGN = 64
 
-GROUP = ((True, 0), (False, 0), (False, 1), (True, 1))
+GROUP = ((False, 0), (True, 0), (False, 1), (True, 1))
 
 
 def tile_list_replay_huber_novelty_kernel(
@@ -41,43 +40,35 @@ def tile_list_replay_huber_novelty_kernel(
     with ExitStack() as ctx:
         lists = ctx.enter_context(tc.tile_pool(name="lists", bufs=1))
         keep = ctx.enter_context(tc.tile_pool(name="keep", bufs=1))
-        ring = ctx.enter_context(tc.tile_pool(name="ring", bufs=SCORE_BUFS))
-        diff_banks = ctx.enter_context(tc.psum_pool(name="diff_banks", bufs=DIFF_BANKS))
-        sum_banks = ctx.enter_context(tc.psum_pool(name="sum_banks", bufs=8 - DIFF_BANKS))
+        banks = ctx.enter_context(tc.psum_pool(name="banks", bufs=1))
 
         idx = lists.tile([P, S // LIST_ROWS], U16, name="idx")
         idx2 = lists.tile([P, S // LIST_ROWS], U16, name="idx2")
 
         tab_sc = keep.tile([P, T // 4], I32, name="tab_sc", tag="second_table", align_bytes=ALIGN)
-        w4_sc_raw = keep.tile([P, PASSES, H // 4], I32, name="w4_sc_raw", align_bytes=ALIGN)
-        v_sc = keep.tile([P, PASSES, S // 4], I32, name="v_sc", align_bytes=ALIGN)
+        w4_sc_raw = keep.tile([P, H // 4], I32, name="w4_sc_raw", align_bytes=ALIGN)
+        planes = keep.tile([P, PASSES, (S + H) // 4], I32, name="planes", align_bytes=ALIGN)
         seed = keep.tile([P, 1], F32, name="seed")
         one = keep.tile([P, 1], F32, name="one")
-        nc.vector.memset(w4_sc_raw[:], 0)
         nc.vector.memset(seed[:], 1.0)
         nc.vector.memset(tab_sc[32:64, :], 0)
         nc.vector.memset(tab_sc[64:P, :], 0)
-        nc.vector.memset(v_sc[:], 0)
+        nc.vector.memset(planes[:], 0)
 
         windows = []
 
-        def new_window(tag, engine, piece):
+        def new_window(tag):
             window = keep.tile([P, T2], F32, name="window%d" % len(windows), tag=tag, align_bytes=ALIGN)
-            for c0 in range(0, T2, piece):
-                engine.memset(window[:, c0 : c0 + piece], 0.0)
+            nc.vector.memset(window[:], 0.0)
             windows.append(window)
 
-        new_window("window0", nc.vector, T2)
+        new_window("window0")
 
-        for quad in range(QUADS):
-            nc.scalar.dma_start(
-                w4_sc_raw[32 * quad : 32 * quad + 4, :, :],
-                w4_scales[:, 4 * quad : 4 * quad + 4, :].rearrange("a r c -> r a c").bitcast(I32),
-            )
+        nc.scalar.dma_start(w4_sc_raw[0:32, :], w4_scales.rearrange("a q c -> q a c").bitcast(I32))
         nc.scalar.activation(one[:], seed[:], ACT.Sqrt)
 
-        def load_w1(a):
-            raw = keep.tile([P, PACK, H], F32, name="w1_raw%d" % a, tag="w1_raw", align_bytes=ALIGN)
+        def load_w1(a, tag):
+            raw = keep.tile([P, PACK, H], F32, name="w1_raw%d" % a, tag=tag, align_bytes=ALIGN)
             nc.sync.dma_start(raw[:], w1[a * K_PASS : (a + 1) * K_PASS, :].rearrange("(p i) c -> p i c", i=PACK))
             return raw[:].rearrange("p i (q t m) -> p t q m i", t=PACK, m=RUN)
 
@@ -88,88 +79,102 @@ def tile_list_replay_huber_novelty_kernel(
 
         nc.sync.dma_start(tab_sc[0:32, :], tab_scales.rearrange("a q t -> q a t").bitcast(I32))
         nc.sync.dma_start(idx[:], offs)
-        nc.sync.dma_start(idx2[:], offs2)
-        w4_raw = keep.tile([P, PASSES, H // 2], I32, name="w4_raw", tag="window1", align_bytes=ALIGN)
-        nc.sync.dma_start(w4_raw[:], w4_words.rearrange("a p c -> p a c").bitcast(I32))
-        w1_first = load_w1(0)
         tab_first = load_table(0, "first_table")
+        nc.sync.dma_start(idx2[:], offs2)
+        w4_raw = keep.tile([P, PASSES, H // 2], I32, name="w4_raw", tag="w4_raw", align_bytes=ALIGN)
+        nc.sync.dma_start(w4_raw[:], w4_words.rearrange("a p c -> p a c").bitcast(I32))
+        w1_first = load_w1(0, "first_w1")
 
         picked_sc = keep.tile([P, S // 4], I32, name="picked_sc", align_bytes=ALIGN)
         nc.vector.tensor_copy(picked_sc[:].bitcast(U8), tab_sc[:].bitcast(U8).indirect(idx[:]))
-        tab_second = load_table(1, "second_table")
+        rows = keep.tile([P, (S + H) // 4], I32, name="rows", align_bytes=ALIGN)
+        nc.vector.tensor_copy(
+            rows[0:32, S // 4 :].rearrange("p (t q w) -> p t q w", t=PACK, w=RUN // 4),
+            w4_sc_raw[0:32, :].rearrange("p (q t w) -> p t q w", t=PACK, w=RUN // 4),
+        )
+        nc.vector.tensor_copy(rows[0:32, 0 : S // 4], picked_sc[0:32, :])
         for quad in range(QUADS):
-            nc.sync.dma_start(v_sc[32 * quad : 32 * quad + 4, :, :], picked_sc[8 * quad : 8 * quad + 8, :])
+            nc.sync.dma_start(planes[32 * quad : 32 * quad + 4, :, :], rows[8 * quad : 8 * quad + 8, :])
+        tab_second = load_table(1, "second_table")
+        new_window("window1")
 
-        w1_bf = [
-            keep.tile([P, PACK, P * PACK], BF16, name="w1_bf%d" % a, tag="w1_bf%d" % a, align_bytes=ALIGN)
-            for a in range(PASSES)
-        ]
-        w1_q = keep.tile([P, PASSES, H], U32, name="w1_q", align_bytes=ALIGN)
-        w1_sc = keep.tile([P, PASSES, H], U8, name="w1_sc", align_bytes=ALIGN)
+        v_q = {}
 
-        def grouped(a, t):
-            return w1_bf[a][:, t, :].rearrange("p (q m i) -> p q m i", m=RUN, i=PACK)
+        def pick_words(a, j0, table, tag):
+            v_q[a, j0] = keep.tile([P, HALF], U32, name="v_q%d_%d" % (a, j0), tag=tag, align_bytes=ALIGN)
+            nc.vector.tensor_copy(v_q[a, j0][:], table.indirect(idx[:, j0 // LIST_ROWS : (j0 + HALF) // LIST_ROWS]))
 
-        for t in range(PACK):
-            nc.scalar.activation(grouped(0, t), w1_first[:, t], ACT.Copy, scale=-1.0)
-        w1_second = load_w1(1)
+        pick_words(0, 0, tab_first, "v_q00")
+        pick_words(0, HALF, tab_first, "v_q01")
+        second_raw = keep.tile([P, PACK * H], F32, name="w1_raw1", tag="first_table", align_bytes=ALIGN)
+        w1_second = []
+        for half in range(2):
+            raw = second_raw[:, half * PACK * H // 2 : (half + 1) * PACK * H // 2].rearrange("p (i c) -> p i c", i=PACK)
+            columns = slice(half * H // 2, (half + 1) * H // 2)
+            nc.sync.dma_start(raw, w1[K_PASS:K, columns].rearrange("(p i) c -> p i c", i=PACK))
+            w1_second.append(raw.rearrange("p i (q t m) -> p t q m i", t=PACK, m=RUN))
 
         w4_q = keep.tile([P, PASSES, H // 2], I32, name="w4_q", align_bytes=ALIGN)
-        w4_sc = keep.tile([P, PASSES, H // 4], I32, name="w4_sc", align_bytes=ALIGN)
         for a in range(PASSES):
             nc.vector.tensor_copy(
                 w4_q[:, a, :].rearrange("p (t q w) -> p t q w", t=PACK, w=RUN // 2),
                 w4_raw[:, a, :].rearrange("p (q t w) -> p t q w", t=PACK, w=RUN // 2),
             )
-            nc.vector.tensor_copy(
-                w4_sc[:, a, :].rearrange("p (t q w) -> p t q w", t=PACK, w=RUN // 4),
-                w4_sc_raw[:, a, :].rearrange("p (q t w) -> p t q w", t=PACK, w=RUN // 4),
-            )
-        nc.vector.quantize_mx(
-            out=w1_q[:, 0, :].bitcast(FP8X4), scales=w1_sc[:, 0, :], in_=w1_bf[0][:].rearrange("p t c -> p (t c)")
-        )
-        new_window("window1", nc.gpsimd, CHUNK)
-        new_window("w1_bf0", nc.vector, T2)
 
-        v_q = [keep.tile([P, S], U32, name="v_q%d" % a, align_bytes=ALIGN) for a in range(PASSES)]
-        nc.vector.tensor_copy(v_q[0][:], tab_first.indirect(idx[:]))
-        w2_raw = keep.tile([P, PACK, N], F32, name="w2_raw", tag="first_table", align_bytes=ALIGN)
+        w1_q = keep.tile([P, PASSES, H], U32, name="w1_q", align_bytes=ALIGN)
+        w1_sc = keep.tile([P, PASSES, H], U8, name="w1_sc", align_bytes=ALIGN)
+
+        def quantise_w1(a, raw, first, width, tag, on_scalar):
+            rounded = keep.tile([P, PACK, width * PACK], BF16, name=tag, tag=tag, align_bytes=ALIGN)
+            for t in range(PACK):
+                grouped = rounded[:, t, :].rearrange("p (q m i) -> p q m i", m=RUN, i=PACK)
+                if t in on_scalar:
+                    nc.scalar.activation(grouped, raw[:, t], ACT.Copy, scale=-1.0)
+                else:
+                    nc.vector.tensor_scalar(grouped, raw[:, t], -1.0, None, MULT)
+            for t in range(PACK):
+                features = slice(t * P + first, t * P + first + width)
+                nc.vector.quantize_mx(
+                    out=w1_q[:, a, features].bitcast(FP8X4), scales=w1_sc[:, a, features], in_=rounded[:, t, :]
+                )
+
+        quantise_w1(0, w1_first, 0, P, "w1_bf0", (1, 3))
+        new_window("w1_bf0")
+        new_window("w4_raw")
+
         w2_rows = w2.rearrange("(q t m) n -> t q m n", t=PACK, m=RUN)
+        early = EARLY_TILES * P
+        later = keep.tile([P, PACK * N + S], F32, name="w2_wgo", tag="first_w1", align_bytes=ALIGN)
+        w2_early = later[:, 0 : PACK * early].rearrange("p (t n) -> p t n", t=PACK)
+        wgo_sb = later[:, PACK * early : PACK * early + S]
         for t in range(PACK):
-            nc.sync.dma_start(w2_raw[:, t, :], w2_rows[t])
-        for j0 in range(0, S, HALF):
-            nc.vector.tensor_copy(
-                v_q[1][:, j0 : j0 + HALF], tab_second.indirect(idx[:, j0 // LIST_ROWS : (j0 + HALF) // LIST_ROWS])
-            )
-        wgo_sb = keep.tile([P, S], F32, name="wgo_sb", tag="second_table", align_bytes=ALIGN)
-        nc.sync.dma_start(wgo_sb[:], wgo)
+            nc.sync.dma_start(w2_early[:, t, :], w2_rows[t][:, :, 0:early])
+        nc.sync.dma_start(wgo_sb, wgo)
+        w2_late = later[:, PACK * early + S :].rearrange("p (t n) -> p t n", t=PACK)
+        for t in range(PACK):
+            nc.sync.dma_start(w2_late[:, t, :], w2_rows[t][:, :, early:N])
 
-        for t in range(PACK):
-            if t % 2 == 0:
-                nc.vector.tensor_scalar(grouped(1, t), w1_second[:, t], -1.0, None, MULT)
-            else:
-                nc.scalar.activation(grouped(1, t), w1_second[:, t], ACT.Copy, scale=-1.0)
-        for t in range(PACK):
-            features = slice(t * P, (t + 1) * P)
-            nc.vector.quantize_mx(
-                out=w1_q[:, 1, features].bitcast(FP8X4), scales=w1_sc[:, 1, features], in_=w1_bf[1][:, t, :]
-            )
+        pick_words(1, 0, tab_second, "v_q10")
+        quantise_w1(1, w1_second[0], 0, P // 2, "w1_bf1", (1, 3))
+        quantise_w1(1, w1_second[1], P // 2, P // 2, "w1_bf2", (3,))
 
         w2_q = keep.tile([P, N], U32, name="w2_q", align_bytes=ALIGN)
         w2_sc = keep.tile([P, N], U8, name="w2_sc", align_bytes=ALIGN)
 
-        def quantise_w2(heads, rounded):
+        def quantise_w2(first, width, raw, on_scalar):
+            heads = slice(first, first + width)
+            rounded = keep.tile([P, width, PACK], BF16, name="w2_bf%d" % first, align_bytes=ALIGN)
+            if on_scalar:
+                nc.scalar.activation(rounded[:], raw.rearrange("p t n -> p n t"), ACT.Copy)
+            else:
+                nc.vector.tensor_copy(
+                    rounded[:].rearrange("p (c i) t -> p c t i", i=4), raw.rearrange("p t (c i) -> p c t i", i=4)
+                )
             nc.vector.quantize_mx(
                 out=w2_q[:, heads].bitcast(FP8X4), scales=w2_sc[:, heads], in_=rounded[:].rearrange("p n t -> p (n t)")
             )
 
-        for first, last in ((0, 2 * P), (2 * P, EARLY_TILES * P)):
-            rounded = keep.tile([P, last - first, PACK], BF16, name="w2_bf%d" % first, align_bytes=ALIGN)
-            nc.vector.tensor_copy(
-                rounded[:].rearrange("p (c i) t -> p c t i", i=4),
-                w2_raw[:, :, first:last].rearrange("p t (c i) -> p c t i", i=4),
-            )
-            quantise_w2(slice(first, last), rounded)
+        quantise_w2(0, early, w2_early, False)
 
         h_bf = [
             keep.tile([P, CHUNK, PACK], BF16, name="h_bf%d" % c, tag="h_bf%d" % c, align_bytes=ALIGN)
@@ -178,53 +183,48 @@ def tile_list_replay_huber_novelty_kernel(
         h_q = keep.tile([P, S], U32, name="h_q", align_bytes=ALIGN)
         h_sc = keep.tile([P, S], U8, name="h_sc", align_bytes=ALIGN)
 
-        def one_pass(diff, j0, t, step):
-            cols = slice(j0, j0 + COLS)
-            online, a = GROUP[step]
-            if online:
-                codes = w1_q[:, a, t * P : (t + 1) * P].bitcast(FP8X4)
-                scales = w1_sc[:, a, t * P : (t + 1) * P]
-            else:
-                codes = w4_q[:, a, t * P // 2 : (t + 1) * P // 2].bitcast(U8).bitcast(FP4X4)
-                scales = w4_sc[:, a, t * P // 4 : (t + 1) * P // 4].bitcast(U8)
-            nc.tensor.matmul_mx(
-                diff[:, t, :],
-                lhsT=codes,
-                lhsT_scale=scales,
-                rhs=v_q[a][:, cols].bitcast(FP8X4),
-                rhs_scale=v_sc[:, a, :].bitcast(U8)[:, cols],
-                start=(step == 0),
-                stop=(step == len(GROUP) - 1),
-            )
-
-        opened = {}
-        for j0 in range(0, DIFF_BANKS * COLS, COLS):
-            opened[j0] = diff_banks.tile([P, PACK, COLS], F32, name="diff", tag="diff")
-            for step in range(len(GROUP) - 1):
-                one_pass(opened[j0], j0, 0, step)
-
         def square_differences(j0):
-            diff = opened[j0] if j0 in opened else diff_banks.tile([P, PACK, COLS], F32, name="diff", tag="diff")
-            for t in range(PACK):
-                done = len(GROUP) - 1 if (j0 in opened and t == 0) else 0
-                for step in range(done, len(GROUP)):
-                    one_pass(diff, j0, t, step)
+            bank = j0 // COLS
+            diff = banks.tile([P, PACK, COLS], F32, name="diff%d" % bank, tag="bank%d" % bank)
+            cols = slice(j0, j0 + COLS)
+            ahead = AHEAD[j0 // CHUNK]
+            order = GROUP[:ahead] + GROUP[-1:] + GROUP[ahead:-1]
+            for step, (online, a) in enumerate(order):
+                values = range(PACK) if j0 < CHUNK else reversed(range(PACK))
+                for count, t in enumerate(values):
+                    if online:
+                        codes = w1_q[:, a, t * P : (t + 1) * P].bitcast(FP8X4)
+                        scales = w1_sc[:, a, t * P : (t + 1) * P]
+                    else:
+                        codes = w4_q[:, a, t * P // 2 : (t + 1) * P // 2].bitcast(U8).bitcast(FP4X4)
+                        scales = planes[:, a, :].bitcast(U8)[:, S + t * P : S + (t + 1) * P]
+                    nc.tensor.matmul_mx(
+                        diff[:, t, :],
+                        lhsT=codes,
+                        lhsT_scale=scales,
+                        rhs=v_q[a, j0 - j0 % HALF][:, j0 % HALF : j0 % HALF + COLS].bitcast(FP8X4),
+                        rhs_scale=planes[:, a, :].bitcast(U8)[:, cols],
+                        start=(step == 0 and count == 0),
+                        stop=(step == len(GROUP) - 1 and count == PACK - 1),
+                    )
             nc.scalar.activation(
                 h_bf[j0 // CHUNK][:, j0 % CHUNK : j0 % CHUNK + COLS, :], diff[:].rearrange("p t j -> p j t"), ACT.Square
             )
 
-        def quantise_h(j0):
-            cols = slice(j0, j0 + CHUNK)
+        def quantise_h(j0, width):
+            cols = slice(j0, j0 + width)
             nc.vector.quantize_mx(
                 out=h_q[:, cols].bitcast(FP8X4),
                 scales=h_sc[:, cols],
-                in_=h_bf[j0 // CHUNK][:].rearrange("p j t -> p (j t)"),
+                in_=h_bf[j0 // CHUNK][:, j0 % CHUNK : j0 % CHUNK + width, :].rearrange("p j t -> p (j t)"),
             )
 
-        def score(n, j0, width):
+        ys = [keep.tile([P, S], F32, name="y%d" % n, align_bytes=ALIGN) for n in range(N // P)]
+
+        def score(n, j0, width, bank):
             cols = slice(j0, j0 + width)
             heads = slice(n * P, (n + 1) * P)
-            x = sum_banks.tile([P, width], F32, name="x", tag="x")
+            x = banks.tile([P, width], F32, name="x%d_%d" % (n, j0), tag="bank%d" % bank)
             nc.tensor.matmul_mx(
                 x[:],
                 lhsT=w2_q[:, heads].bitcast(FP8X4),
@@ -234,36 +234,38 @@ def tile_list_replay_huber_novelty_kernel(
                 start=True,
                 stop=True,
             )
-            y = ring.tile([P, width], F32, name="y", tag="y")
-            nc.scalar.activation(y[:], x[:], ACT.Sqrt, bias=one[:])
-            return y
+            nc.scalar.activation(ys[n][:, cols], x[:], ACT.Sqrt, bias=one[:])
 
-        def place(n, j0, width, y):
+        def place(n, j0, width):
             places = idx2[:, j0 // LIST_ROWS : (j0 + width) // LIST_ROWS]
-            nc.vector.tensor_tensor(windows[n][:].indirect(places), y[:], wgo_sb[:, j0 : j0 + width], MULT)
+            nc.vector.tensor_tensor(
+                windows[n][:].indirect(places), ys[n][:, j0 : j0 + width], wgo_sb[:, j0 : j0 + width], MULT
+            )
             if j0 + width == S:
                 nc.sync.dma_start(out[n * P : (n + 1) * P, :], windows[n][:])
 
-        square_differences(0)
-        square_differences(COLS)
-        quantise_h(0)
+        for j0 in range(0, CHUNK, COLS):
+            square_differences(j0)
+            quantise_h(j0, COLS)
+        pick_words(1, HALF, tab_second, "h_bf0")
+        score(0, 0, COLS, 0)
+        score(0, COLS, COLS, 1)
         for j0 in range(0, S, CHUNK):
             ahead = j0 + CHUNK
-            scores = [score(0, j0, CHUNK)]
             if ahead < S:
                 square_differences(ahead)
                 square_differences(ahead + COLS)
-            scores += [score(n, j0, CHUNK) for n in range(1, EARLY_TILES)]
-            place(0, j0, CHUNK, scores[0])
+            for n in range(EARLY_TILES):
+                if n > 0 or j0 > 0:
+                    score(n, j0, CHUNK, (ahead // COLS + n) % 8)
+            place(0, j0, CHUNK)
             if ahead < S:
-                quantise_h(ahead)
+                quantise_h(ahead, CHUNK)
             for n in range(1, EARLY_TILES):
-                place(n, j0, CHUNK, scores[n])
+                place(n, j0, CHUNK)
 
-        heads = slice(EARLY_TILES * P, N)
-        rounded = keep.tile([P, P, PACK], BF16, name="w2_last", tag="h_bf1", align_bytes=ALIGN)
-        nc.scalar.activation(rounded[:], w2_raw[:, :, heads].rearrange("p t n -> p n t"), ACT.Copy)
-        quantise_w2(heads, rounded)
-        new_window("first_table", nc.gpsimd, CHUNK)
-        for j0 in range(0, S, HALF):
-            place(EARLY_TILES, j0, HALF, score(EARLY_TILES, j0, HALF))
+        quantise_w2(early, N - early, w2_late, True)
+        for n in range(EARLY_TILES, N // P):
+            for j0 in range(0, S, HALF):
+                score(n, j0, HALF, 2 + 2 * (j0 // HALF))
+            place(n, 0, S)

@@ -51,8 +51,7 @@ def tile_list_replay_huber_novelty_kernel(
         seed = keep.tile([P, 1], F32, name="seed")
         one = keep.tile([P, 1], F32, name="one")
         nc.vector.memset(seed[:], 1.0)
-        nc.vector.memset(tab_sc[32:64, :], 0)
-        nc.vector.memset(tab_sc[64:P, :], 0)
+        nc.vector.memset(tab_sc[0:96, :], 0)
         nc.vector.memset(planes[:], 0)
 
         windows = []
@@ -64,7 +63,7 @@ def tile_list_replay_huber_novelty_kernel(
 
         new_window("window0")
 
-        nc.scalar.dma_start(w4_sc_raw[0:32, :], w4_scales.rearrange("a q c -> q a c").bitcast(I32))
+        nc.scalar.dma_start(w4_sc_raw[96:P, :], w4_scales.rearrange("a q c -> q a c").bitcast(I32))
         nc.scalar.activation(one[:], seed[:], ACT.Sqrt)
 
         def load_w1(a, tag):
@@ -77,11 +76,11 @@ def tile_list_replay_huber_novelty_kernel(
             nc.sync.dma_start(words[:], tab_words[a].rearrange("p t i -> p (t i)").bitcast(I32))
             return words[:].bitcast(U32)
 
-        nc.sync.dma_start(tab_sc[0:32, :], tab_scales.rearrange("a q t -> q a t").bitcast(I32))
+        nc.sync.dma_start(tab_sc[96:P, :], tab_scales.rearrange("a q t -> q a t").bitcast(I32))
         nc.sync.dma_start(idx[:], offs)
         tab_first = load_table(0, "first_table")
         nc.sync.dma_start(idx2[:], offs2)
-        w4_raw = keep.tile([P, PASSES, H // 2], I32, name="w4_raw", tag="w4_raw", align_bytes=ALIGN)
+        w4_raw = keep.tile([P, PASSES, H // 2], I32, name="w4_raw", align_bytes=ALIGN)
         nc.sync.dma_start(w4_raw[:], w4_words.rearrange("a p c -> p a c").bitcast(I32))
         w1_first = load_w1(0, "first_w1")
 
@@ -89,14 +88,13 @@ def tile_list_replay_huber_novelty_kernel(
         nc.vector.tensor_copy(picked_sc[:].bitcast(U8), tab_sc[:].bitcast(U8).indirect(idx[:]))
         rows = keep.tile([P, (S + H) // 4], I32, name="rows", align_bytes=ALIGN)
         nc.vector.tensor_copy(
-            rows[0:32, S // 4 :].rearrange("p (t q w) -> p t q w", t=PACK, w=RUN // 4),
-            w4_sc_raw[0:32, :].rearrange("p (q t w) -> p t q w", t=PACK, w=RUN // 4),
+            rows[96:P, S // 4 :].rearrange("p (t q w) -> p t q w", t=PACK, w=RUN // 4),
+            w4_sc_raw[96:P, :].rearrange("p (q t w) -> p t q w", t=PACK, w=RUN // 4),
         )
-        nc.vector.tensor_copy(rows[0:32, 0 : S // 4], picked_sc[0:32, :])
+        nc.vector.tensor_copy(rows[96:P, 0 : S // 4], picked_sc[96:P, :])
         for quad in range(QUADS):
-            nc.sync.dma_start(planes[32 * quad : 32 * quad + 4, :, :], rows[8 * quad : 8 * quad + 8, :])
+            nc.sync.dma_start(planes[32 * quad : 32 * quad + 4, :, :], rows[96 + 8 * quad : 96 + 8 * quad + 8, :])
         tab_second = load_table(1, "second_table")
-        new_window("window1")
 
         v_q = {}
 
@@ -125,9 +123,12 @@ def tile_list_replay_huber_novelty_kernel(
         w1_sc = keep.tile([P, PASSES, H], U8, name="w1_sc", align_bytes=ALIGN)
 
         def quantise_w1(a, raw, first, width, tag, on_scalar):
-            rounded = keep.tile([P, PACK, width * PACK], BF16, name=tag, tag=tag, align_bytes=ALIGN)
+            rounded = [
+                keep.tile([P, width * PACK], BF16, name="%s_%d" % (tag, t), tag="%s_%d" % (tag, t), align_bytes=ALIGN)
+                for t in range(PACK)
+            ]
             for t in range(PACK):
-                grouped = rounded[:, t, :].rearrange("p (q m i) -> p q m i", m=RUN, i=PACK)
+                grouped = rounded[t][:].rearrange("p (q m i) -> p q m i", m=RUN, i=PACK)
                 if t in on_scalar:
                     nc.scalar.activation(grouped, raw[:, t], ACT.Copy, scale=-1.0)
                 else:
@@ -135,12 +136,13 @@ def tile_list_replay_huber_novelty_kernel(
             for t in range(PACK):
                 features = slice(t * P + first, t * P + first + width)
                 nc.vector.quantize_mx(
-                    out=w1_q[:, a, features].bitcast(FP8X4), scales=w1_sc[:, a, features], in_=rounded[:, t, :]
+                    out=w1_q[:, a, features].bitcast(FP8X4), scales=w1_sc[:, a, features], in_=rounded[t][:]
                 )
 
         quantise_w1(0, w1_first, 0, P, "w1_bf0", (1, 3))
-        new_window("w1_bf0")
-        new_window("w4_raw")
+        new_window("w1_bf0_2")
+        new_window("w1_bf0_3")
+        windows.append(windows[0])
 
         w2_rows = w2.rearrange("(q t m) n -> t q m n", t=PACK, m=RUN)
         early = EARLY_TILES * P

@@ -40,14 +40,15 @@ def tile_list_replay_huber_novelty_kernel(
     with ExitStack() as ctx:
         lists = ctx.enter_context(tc.tile_pool(name="lists", bufs=1))
         keep = ctx.enter_context(tc.tile_pool(name="keep", bufs=1))
+        staged = ctx.enter_context(tc.tile_pool(name="staged", bufs=1))
         banks = ctx.enter_context(tc.psum_pool(name="banks", bufs=1))
 
         idx = lists.tile([P, S // LIST_ROWS], U16, name="idx")
         idx2 = lists.tile([P, S // LIST_ROWS], U16, name="idx2")
 
-        tab_sc = keep.tile([P, T // 4], I32, name="tab_sc", tag="second_table", align_bytes=ALIGN)
+        tab_sc = keep.tile([P, T // 4], I32, name="tab_sc", align_bytes=ALIGN)
         w4_sc_raw = keep.tile([P, H // 4], I32, name="w4_sc_raw", align_bytes=ALIGN)
-        planes = keep.tile([P, PASSES, (S + H) // 4], I32, name="planes", align_bytes=ALIGN)
+        planes = keep.tile([P, 2 * (H + HALF) // 4], I32, name="planes", align_bytes=ALIGN)
         seed = keep.tile([P, 1], F32, name="seed")
         one = keep.tile([P, 1], F32, name="one")
         nc.vector.memset(seed[:], 1.0)
@@ -63,38 +64,53 @@ def tile_list_replay_huber_novelty_kernel(
 
         new_window("window0")
 
-        nc.scalar.dma_start(w4_sc_raw[96:P, :], w4_scales.rearrange("a q c -> q a c").bitcast(I32))
+        nc.scalar.dma_start(w4_sc_raw[96:P, :], w4_scales.rearrange("a q c -> (a q) c").bitcast(I32))
         nc.scalar.activation(one[:], seed[:], ACT.Sqrt)
 
-        def load_w1(a, tag):
-            raw = keep.tile([P, PACK, H], F32, name="w1_raw%d" % a, tag=tag, align_bytes=ALIGN)
+        def load_w1(a):
+            raw = staged.tile([P, PACK, H], F32, name="w1_raw%d" % a, offset=0, align_bytes=ALIGN)
             nc.sync.dma_start(raw[:], w1[a * K_PASS : (a + 1) * K_PASS, :].rearrange("(p i) c -> p i c", i=PACK))
             return raw[:].rearrange("p i (q t m) -> p t q m i", t=PACK, m=RUN)
 
-        def load_table(a, tag):
-            words = keep.tile([P, T], I32, name="tab%d" % a, tag=tag, align_bytes=ALIGN)
+        def load_table(a, words):
             nc.sync.dma_start(words[:], tab_words[a].rearrange("p t i -> p (t i)").bitcast(I32))
             return words[:].bitcast(U32)
 
-        nc.sync.dma_start(tab_sc[96:P, :], tab_scales.rearrange("a q t -> q a t").bitcast(I32))
+        nc.sync.dma_start(tab_sc[96:P, :], tab_scales.rearrange("a q t -> (a q) t").bitcast(I32))
         nc.sync.dma_start(idx[:], offs)
-        tab_first = load_table(0, "first_table")
-        nc.sync.dma_start(idx2[:], offs2)
-        w4_raw = keep.tile([P, PASSES, H // 2], I32, name="w4_raw", align_bytes=ALIGN)
+        w4_raw = keep.tile([P, PASSES, H // 2], I32, name="w4_raw", tag="w4_raw", align_bytes=ALIGN)
         nc.sync.dma_start(w4_raw[:], w4_words.rearrange("a p c -> p a c").bitcast(I32))
-        w1_first = load_w1(0, "first_w1")
+        first_words = keep.tile([P, T], I32, name="tab0", tag="first_table", align_bytes=ALIGN)
+        tab_first = load_table(0, first_words)
+        nc.sync.dma_start(idx2[:], offs2)
+        w1_first = load_w1(0)
 
-        picked_sc = keep.tile([P, S // 4], I32, name="picked_sc", align_bytes=ALIGN)
+        picked_sc = keep.tile([P, S // 4], I32, name="picked_sc", tag="second_table", align_bytes=ALIGN)
         nc.vector.tensor_copy(picked_sc[:].bitcast(U8), tab_sc[:].bitcast(U8).indirect(idx[:]))
         rows = keep.tile([P, (S + H) // 4], I32, name="rows", align_bytes=ALIGN)
         nc.vector.tensor_copy(
-            rows[96:P, S // 4 :].rearrange("p (t q w) -> p t q w", t=PACK, w=RUN // 4),
+            rows[96:P, 0 : H // 4].rearrange("p (t q w) -> p t q w", t=PACK, w=RUN // 4),
             w4_sc_raw[96:P, :].rearrange("p (q t w) -> p t q w", t=PACK, w=RUN // 4),
         )
-        nc.vector.tensor_copy(rows[96:P, 0 : S // 4], picked_sc[96:P, :])
-        for quad in range(QUADS):
-            nc.sync.dma_start(planes[32 * quad : 32 * quad + 4, :, :], rows[96 + 8 * quad : 96 + 8 * quad + 8, :])
-        tab_second = load_table(1, "second_table")
+        nc.vector.tensor_copy(rows[96:P, H // 4 :], picked_sc[96:P, :])
+
+        def move_scale_rows(a, plane, first, last):
+            for r in range(4):
+                nc.sync.dma_start(plane[r:P:32, :], rows[96 + 16 * a + r : 112 + 16 * a : 4, first // 4 : last // 4])
+
+        plane_first = planes[:, 0 : (H + HALF) // 4]
+        plane_second = planes[:, (H + HALF) // 4 :]
+        move_scale_rows(0, plane_first, 0, H + HALF)
+        second_words = keep.tile([P, T], I32, name="tab1", tag="second_table", align_bytes=ALIGN)
+        tab_second = load_table(1, second_words)
+        move_scale_rows(1, plane_second, 0, H + HALF)
+
+        w4_q = keep.tile([P, PASSES, H // 2], I32, name="w4_q", align_bytes=ALIGN)
+        for a in range(PASSES):
+            nc.vector.tensor_copy(
+                w4_q[:, a, :].rearrange("p (t q w) -> p t q w", t=PACK, w=RUN // 2),
+                w4_raw[:, a, :].rearrange("p (q t w) -> p t q w", t=PACK, w=RUN // 2),
+            )
 
         v_q = {}
 
@@ -111,13 +127,6 @@ def tile_list_replay_huber_novelty_kernel(
             columns = slice(half * H // 2, (half + 1) * H // 2)
             nc.sync.dma_start(raw, w1[K_PASS:K, columns].rearrange("(p i) c -> p i c", i=PACK))
             w1_second.append(raw.rearrange("p i (q t m) -> p t q m i", t=PACK, m=RUN))
-
-        w4_q = keep.tile([P, PASSES, H // 2], I32, name="w4_q", align_bytes=ALIGN)
-        for a in range(PASSES):
-            nc.vector.tensor_copy(
-                w4_q[:, a, :].rearrange("p (t q w) -> p t q w", t=PACK, w=RUN // 2),
-                w4_raw[:, a, :].rearrange("p (q t w) -> p t q w", t=PACK, w=RUN // 2),
-            )
 
         w1_q = keep.tile([P, PASSES, H], U32, name="w1_q", align_bytes=ALIGN)
         w1_sc = keep.tile([P, PASSES, H], U8, name="w1_sc", align_bytes=ALIGN)
@@ -139,26 +148,33 @@ def tile_list_replay_huber_novelty_kernel(
                     out=w1_q[:, a, features].bitcast(FP8X4), scales=w1_sc[:, a, features], in_=rounded[t][:]
                 )
 
+        new_window("w4_raw")
         quantise_w1(0, w1_first, 0, P, "w1_bf0", (1, 3))
-        new_window("w1_bf0_2")
         new_window("w1_bf0_3")
         windows.append(windows[0])
 
         w2_rows = w2.rearrange("(q t m) n -> t q m n", t=PACK, m=RUN)
         early = EARLY_TILES * P
-        later = keep.tile([P, PACK * N + S], F32, name="w2_wgo", tag="first_w1", align_bytes=ALIGN)
+        later = staged.tile([P, PACK * early + S], F32, name="w2_wgo", offset=S, align_bytes=ALIGN)
         w2_early = later[:, 0 : PACK * early].rearrange("p (t n) -> p t n", t=PACK)
-        wgo_sb = later[:, PACK * early : PACK * early + S]
+        wgo_sb = later[:, PACK * early :]
         for t in range(PACK):
             nc.sync.dma_start(w2_early[:, t, :], w2_rows[t][:, :, 0:early])
         nc.sync.dma_start(wgo_sb, wgo)
-        w2_late = later[:, PACK * early + S :].rearrange("p (t n) -> p t n", t=PACK)
-        for t in range(PACK):
-            nc.sync.dma_start(w2_late[:, t, :], w2_rows[t][:, :, early:N])
+        plane_last = staged.tile([P, S // 4], I32, name="plane_last", offset=0, align_bytes=ALIGN)
+        nc.vector.memset(plane_last[:], 0)
+        for a in range(PASSES):
+            move_scale_rows(a, plane_last[:, a * HALF // 4 : (a + 1) * HALF // 4], H + HALF, H + S)
 
         pick_words(1, 0, tab_second, "v_q10")
         quantise_w1(1, w1_second[0], 0, P // 2, "w1_bf1", (1, 3))
         quantise_w1(1, w1_second[1], P // 2, P // 2, "w1_bf2", (3,))
+        w4_scale_bytes = [plane.bitcast(U8)[:, 0:H] for plane in (plane_first, plane_second)]
+
+        def v_scale_bytes(a, j0):
+            if j0 >= HALF:
+                return plane_last[:].bitcast(U8)[:, (a - 1) * HALF + j0 : (a - 1) * HALF + j0 + COLS]
+            return (plane_first, plane_second)[a].bitcast(U8)[:, H + j0 : H + j0 + COLS]
 
         w2_q = keep.tile([P, N], U32, name="w2_q", align_bytes=ALIGN)
         w2_sc = keep.tile([P, N], U8, name="w2_sc", align_bytes=ALIGN)
@@ -188,7 +204,6 @@ def tile_list_replay_huber_novelty_kernel(
         def square_differences(j0):
             bank = j0 // COLS
             diff = banks.tile([P, PACK, COLS], F32, name="diff%d" % bank, tag="bank%d" % bank)
-            cols = slice(j0, j0 + COLS)
             ahead = AHEAD[j0 // CHUNK]
             order = GROUP[:ahead] + GROUP[-1:] + GROUP[ahead:-1]
             for step, (online, a) in enumerate(order):
@@ -199,13 +214,13 @@ def tile_list_replay_huber_novelty_kernel(
                         scales = w1_sc[:, a, t * P : (t + 1) * P]
                     else:
                         codes = w4_q[:, a, t * P // 2 : (t + 1) * P // 2].bitcast(U8).bitcast(FP4X4)
-                        scales = planes[:, a, :].bitcast(U8)[:, S + t * P : S + (t + 1) * P]
+                        scales = w4_scale_bytes[a][:, t * P : (t + 1) * P]
                     nc.tensor.matmul_mx(
                         diff[:, t, :],
                         lhsT=codes,
                         lhsT_scale=scales,
                         rhs=v_q[a, j0 - j0 % HALF][:, j0 % HALF : j0 % HALF + COLS].bitcast(FP8X4),
-                        rhs_scale=planes[:, a, :].bitcast(U8)[:, cols],
+                        rhs_scale=v_scale_bytes(a, j0),
                         start=(step == 0 and count == 0),
                         stop=(step == len(GROUP) - 1 and count == PACK - 1),
                     )
@@ -249,6 +264,9 @@ def tile_list_replay_huber_novelty_kernel(
         for j0 in range(0, CHUNK, COLS):
             square_differences(j0)
             quantise_h(j0, COLS)
+        w2_late = keep.tile([P, PACK, N - early], F32, name="w2_late", tag="w1_bf2_3", align_bytes=ALIGN)
+        for t in range(PACK):
+            nc.sync.dma_start(w2_late[:, t, :], w2_rows[t][:, :, early:N])
         pick_words(1, HALF, tab_second, "h_bf0")
         score(0, 0, COLS, 0)
         score(0, COLS, COLS, 1)
@@ -266,7 +284,7 @@ def tile_list_replay_huber_novelty_kernel(
             for n in range(1, EARLY_TILES):
                 place(n, j0, CHUNK)
 
-        quantise_w2(early, N - early, w2_late, True)
+        quantise_w2(early, N - early, w2_late[:], True)
         for n in range(EARLY_TILES, N // P):
             for j0 in range(0, S, HALF):
                 score(n, j0, HALF, 2 + 2 * (j0 // HALF))

@@ -19,7 +19,13 @@ MULT = mybir.AluOpType.mult
 P = 128
 PACK = 4
 RUN = 8
-QUADS = 4
+QUAD = 32
+QUAD_ROWS = 4
+BLOCKS = 16
+ROWS_AT = 96
+WORD = 4
+BANKS = 8
+LINE = 4
 K_PASS = P * PACK
 PASSES = K // K_PASS
 LIST_ROWS = 16
@@ -46,13 +52,13 @@ def tile_list_replay_huber_novelty_kernel(
         idx = lists.tile([P, S // LIST_ROWS], U16, name="idx")
         idx2 = lists.tile([P, S // LIST_ROWS], U16, name="idx2")
 
-        tab_sc = keep.tile([P, T // 4], I32, name="tab_sc", align_bytes=ALIGN)
-        w4_sc_raw = keep.tile([P, H // 4], I32, name="w4_sc_raw", align_bytes=ALIGN)
-        planes = keep.tile([P, 2 * (H + HALF) // 4], I32, name="planes", align_bytes=ALIGN)
+        tab_sc = keep.tile([P, T // WORD], I32, name="tab_sc", align_bytes=ALIGN)
+        w4_sc_raw = keep.tile([P, H // WORD], I32, name="w4_sc_raw", align_bytes=ALIGN)
+        planes = keep.tile([P, PASSES * (H + HALF) // WORD], I32, name="planes", align_bytes=ALIGN)
         seed = keep.tile([P, 1], F32, name="seed")
         one = keep.tile([P, 1], F32, name="one")
         nc.vector.memset(seed[:], 1.0)
-        nc.vector.memset(tab_sc[0:96, :], 0)
+        nc.vector.memset(tab_sc[0:ROWS_AT, :], 0)
         nc.vector.memset(planes[:], 0)
 
         windows = []
@@ -64,42 +70,44 @@ def tile_list_replay_huber_novelty_kernel(
 
         new_window("window0")
 
-        nc.scalar.dma_start(w4_sc_raw[96:P, :], w4_scales.rearrange("a q c -> (a q) c").bitcast(I32))
+        nc.scalar.dma_start(w4_sc_raw[ROWS_AT:P, :], w4_scales.rearrange("a q c -> (a q) c").bitcast(I32))
         nc.scalar.activation(one[:], seed[:], ACT.Sqrt)
 
-        def load_w1(a):
-            raw = staged.tile([P, PACK, H], F32, name="w1_raw%d" % a, offset=0, align_bytes=ALIGN)
-            nc.sync.dma_start(raw[:], w1[a * K_PASS : (a + 1) * K_PASS, :].rearrange("(p i) c -> p i c", i=PACK))
-            return raw[:].rearrange("p i (q t m) -> p t q m i", t=PACK, m=RUN)
+        def load_w1(raw, a, columns):
+            nc.sync.dma_start(raw, w1[a * K_PASS : (a + 1) * K_PASS, columns].rearrange("(p i) c -> p i c", i=PACK))
+            return raw.rearrange("p i (q t m) -> p t q m i", t=PACK, m=RUN)
 
         def load_table(a, words):
             nc.sync.dma_start(words[:], tab_words[a].rearrange("p t i -> p (t i)").bitcast(I32))
             return words[:].bitcast(U32)
 
-        nc.sync.dma_start(tab_sc[96:P, :], tab_scales.rearrange("a q t -> (a q) t").bitcast(I32))
+        nc.sync.dma_start(tab_sc[ROWS_AT:P, :], tab_scales.rearrange("a q t -> (a q) t").bitcast(I32))
         nc.sync.dma_start(idx[:], offs)
         w4_raw = keep.tile([P, PASSES, H // 2], I32, name="w4_raw", tag="w4_raw", align_bytes=ALIGN)
         nc.sync.dma_start(w4_raw[:], w4_words.rearrange("a p c -> p a c").bitcast(I32))
         first_words = keep.tile([P, T], I32, name="tab0", tag="first_table", align_bytes=ALIGN)
         tab_first = load_table(0, first_words)
         nc.sync.dma_start(idx2[:], offs2)
-        w1_first = load_w1(0)
+        first_raw = staged.tile([P, PACK, H], F32, name="w1_raw0", offset=0, align_bytes=ALIGN)
+        w1_first = load_w1(first_raw[:], 0, slice(0, H))
 
-        picked_sc = keep.tile([P, S // 4], I32, name="picked_sc", tag="second_table", align_bytes=ALIGN)
+        picked_sc = keep.tile([P, S // WORD], I32, name="picked_sc", tag="second_table", align_bytes=ALIGN)
         nc.vector.tensor_copy(picked_sc[:].bitcast(U8), tab_sc[:].bitcast(U8).indirect(idx[:]))
-        rows = keep.tile([P, (S + H) // 4], I32, name="rows", align_bytes=ALIGN)
+        rows = keep.tile([P, (S + H) // WORD], I32, name="rows", align_bytes=ALIGN)
         nc.vector.tensor_copy(
-            rows[96:P, 0 : H // 4].rearrange("p (t q w) -> p t q w", t=PACK, w=RUN // 4),
-            w4_sc_raw[96:P, :].rearrange("p (q t w) -> p t q w", t=PACK, w=RUN // 4),
+            rows[ROWS_AT:P, 0 : H // WORD].rearrange("p (t q w) -> p t q w", t=PACK, w=RUN // WORD),
+            w4_sc_raw[ROWS_AT:P, :].rearrange("p (q t w) -> p t q w", t=PACK, w=RUN // WORD),
         )
-        nc.vector.tensor_copy(rows[96:P, H // 4 :], picked_sc[96:P, :])
+        nc.vector.tensor_copy(rows[ROWS_AT:P, H // WORD :], picked_sc[ROWS_AT:P, :])
 
         def move_scale_rows(a, plane, first, last):
-            for r in range(4):
-                nc.sync.dma_start(plane[r:P:32, :], rows[96 + 16 * a + r : 112 + 16 * a : 4, first // 4 : last // 4])
+            start = ROWS_AT + BLOCKS * a
+            for r in range(QUAD_ROWS):
+                source = rows[start + r : start + BLOCKS : QUAD_ROWS, first // WORD : last // WORD]
+                nc.sync.dma_start(plane[r:P:QUAD, :], source)
 
-        plane_first = planes[:, 0 : (H + HALF) // 4]
-        plane_second = planes[:, (H + HALF) // 4 :]
+        plane_first = planes[:, 0 : (H + HALF) // WORD]
+        plane_second = planes[:, (H + HALF) // WORD :]
         move_scale_rows(0, plane_first, 0, H + HALF)
         second_words = keep.tile([P, T], I32, name="tab1", tag="second_table", align_bytes=ALIGN)
         tab_second = load_table(1, second_words)
@@ -124,9 +132,7 @@ def tile_list_replay_huber_novelty_kernel(
         w1_second = []
         for half in range(2):
             raw = second_raw[:, half * PACK * H // 2 : (half + 1) * PACK * H // 2].rearrange("p (i c) -> p i c", i=PACK)
-            columns = slice(half * H // 2, (half + 1) * H // 2)
-            nc.sync.dma_start(raw, w1[K_PASS:K, columns].rearrange("(p i) c -> p i c", i=PACK))
-            w1_second.append(raw.rearrange("p i (q t m) -> p t q m i", t=PACK, m=RUN))
+            w1_second.append(load_w1(raw, 1, slice(half * H // 2, (half + 1) * H // 2)))
 
         w1_q = keep.tile([P, PASSES, H], U32, name="w1_q", align_bytes=ALIGN)
         w1_sc = keep.tile([P, PASSES, H], U8, name="w1_sc", align_bytes=ALIGN)
@@ -161,19 +167,20 @@ def tile_list_replay_huber_novelty_kernel(
         for t in range(PACK):
             nc.sync.dma_start(w2_early[:, t, :], w2_rows[t][:, :, 0:early])
         nc.sync.dma_start(wgo_sb, wgo)
-        plane_last = staged.tile([P, S // 4], I32, name="plane_last", offset=0, align_bytes=ALIGN)
-        nc.vector.memset(plane_last[:], 0)
+        plane_late = staged.tile([P, S // WORD], I32, name="plane_late", offset=0, align_bytes=ALIGN)
+        nc.vector.memset(plane_late[:], 0)
         for a in range(PASSES):
-            move_scale_rows(a, plane_last[:, a * HALF // 4 : (a + 1) * HALF // 4], H + HALF, H + S)
+            move_scale_rows(a, plane_late[:, a * HALF // WORD : (a + 1) * HALF // WORD], H + HALF, H + S)
 
         pick_words(1, 0, tab_second, "v_q10")
         quantise_w1(1, w1_second[0], 0, P // 2, "w1_bf1", (1, 3))
         quantise_w1(1, w1_second[1], P // 2, P // 2, "w1_bf2", (3,))
+        pick_words(1, HALF, tab_second, "w1_bf2_3")
         w4_scale_bytes = [plane.bitcast(U8)[:, 0:H] for plane in (plane_first, plane_second)]
 
         def v_scale_bytes(a, j0):
             if j0 >= HALF:
-                return plane_last[:].bitcast(U8)[:, (a - 1) * HALF + j0 : (a - 1) * HALF + j0 + COLS]
+                return plane_late[:].bitcast(U8)[:, (a - 1) * HALF + j0 : (a - 1) * HALF + j0 + COLS]
             return (plane_first, plane_second)[a].bitcast(U8)[:, H + j0 : H + j0 + COLS]
 
         w2_q = keep.tile([P, N], U32, name="w2_q", align_bytes=ALIGN)
@@ -186,7 +193,7 @@ def tile_list_replay_huber_novelty_kernel(
                 nc.scalar.activation(rounded[:], raw.rearrange("p t n -> p n t"), ACT.Copy)
             else:
                 nc.vector.tensor_copy(
-                    rounded[:].rearrange("p (c i) t -> p c t i", i=4), raw.rearrange("p t (c i) -> p c t i", i=4)
+                    rounded[:].rearrange("p (c n) t -> p c t n", n=LINE), raw.rearrange("p t (c n) -> p c t n", n=LINE)
                 )
             nc.vector.quantize_mx(
                 out=w2_q[:, heads].bitcast(FP8X4), scales=w2_sc[:, heads], in_=rounded[:].rearrange("p n t -> p (n t)")
@@ -204,8 +211,8 @@ def tile_list_replay_huber_novelty_kernel(
         def square_differences(j0):
             bank = j0 // COLS
             diff = banks.tile([P, PACK, COLS], F32, name="diff%d" % bank, tag="bank%d" % bank)
-            ahead = AHEAD[j0 // CHUNK]
-            order = GROUP[:ahead] + GROUP[-1:] + GROUP[ahead:-1]
+            before = AHEAD[j0 // CHUNK]
+            order = GROUP[:before] + GROUP[-1:] + GROUP[before:-1]
             for step, (online, a) in enumerate(order):
                 values = range(PACK) if j0 < CHUNK else reversed(range(PACK))
                 for count, t in enumerate(values):
@@ -264,23 +271,22 @@ def tile_list_replay_huber_novelty_kernel(
         for j0 in range(0, CHUNK, COLS):
             square_differences(j0)
             quantise_h(j0, COLS)
-        w2_late = keep.tile([P, PACK, N - early], F32, name="w2_late", tag="w1_bf2_3", align_bytes=ALIGN)
+        w2_late = keep.tile([P, PACK, N - early], F32, name="w2_late", tag="h_bf0", align_bytes=ALIGN)
         for t in range(PACK):
             nc.sync.dma_start(w2_late[:, t, :], w2_rows[t][:, :, early:N])
-        pick_words(1, HALF, tab_second, "h_bf0")
         score(0, 0, COLS, 0)
         score(0, COLS, COLS, 1)
         for j0 in range(0, S, CHUNK):
-            ahead = j0 + CHUNK
-            if ahead < S:
-                square_differences(ahead)
-                square_differences(ahead + COLS)
+            following = j0 + CHUNK
+            if following < S:
+                square_differences(following)
+                square_differences(following + COLS)
             for n in range(EARLY_TILES):
                 if n > 0 or j0 > 0:
-                    score(n, j0, CHUNK, (ahead // COLS + n) % 8)
+                    score(n, j0, CHUNK, (following // COLS + n) % BANKS)
             place(0, j0, CHUNK)
-            if ahead < S:
-                quantise_h(ahead, CHUNK)
+            if following < S:
+                quantise_h(following, CHUNK)
             for n in range(1, EARLY_TILES):
                 place(n, j0, CHUNK)
 

@@ -18,11 +18,11 @@ MULT = mybir.AluOpType.mult
 
 P = 128
 PACK = 4
-RUN = 8
 QUAD = 32
 QUAD_ROWS = 4
 BLOCKS = 16
-ROWS_AT = 96
+ROWS_AT = 32
+ROWS_STEP = 2
 WORD = 4
 BANKS = 8
 LINE = 4
@@ -34,6 +34,7 @@ CHUNK = 256
 HALF = 512
 AHEAD = (3, 2, 2, 0)
 EARLY_TILES = 2
+TABLE_AT = 8128
 ALIGN = 64
 
 GROUP = ((False, 0), (True, 0), (False, 1), (True, 1))
@@ -46,78 +47,90 @@ def tile_list_replay_huber_novelty_kernel(
     with ExitStack() as ctx:
         lists = ctx.enter_context(tc.tile_pool(name="lists", bufs=1))
         keep = ctx.enter_context(tc.tile_pool(name="keep", bufs=1))
+        table = ctx.enter_context(tc.tile_pool(name="table", bufs=1))
         staged = ctx.enter_context(tc.tile_pool(name="staged", bufs=1))
         banks = ctx.enter_context(tc.psum_pool(name="banks", bufs=1))
 
         idx = lists.tile([P, S // LIST_ROWS], U16, name="idx")
         idx2 = lists.tile([P, S // LIST_ROWS], U16, name="idx2")
 
-        tab_sc = keep.tile([P, T // WORD], I32, name="tab_sc", align_bytes=ALIGN)
-        w4_sc_raw = keep.tile([P, H // WORD], I32, name="w4_sc_raw", align_bytes=ALIGN)
+        tab_sc = keep.tile([P, T // WORD], I32, name="tab_sc", tag="tab_sc", align_bytes=ALIGN)
+        w4_sc_raw = keep.tile([P, H // WORD], I32, name="w4_sc_raw", tag="w4_raw", align_bytes=ALIGN)
         planes = keep.tile([P, PASSES * (H + HALF) // WORD], I32, name="planes", align_bytes=ALIGN)
-        seed = keep.tile([P, 1], F32, name="seed")
+        seed = table.tile([P, 1], F32, name="seed", offset=TABLE_AT, align_bytes=ALIGN)
         one = keep.tile([P, 1], F32, name="one")
         nc.vector.memset(seed[:], 1.0)
-        nc.vector.memset(tab_sc[0:ROWS_AT, :], 0)
+        nc.vector.memset(tab_sc[:], 0)
+        nc.vector.memset(w4_sc_raw[:], 0)
         nc.vector.memset(planes[:], 0)
 
         windows = []
 
         def new_window(tag):
-            window = keep.tile([P, T2], F32, name="window%d" % len(windows), tag=tag, align_bytes=ALIGN)
+            if tag is None:
+                window = table.tile([P, T2], F32, name="window2", offset=0, align_bytes=ALIGN)
+            else:
+                window = keep.tile([P, T2], F32, name="window%d" % len(windows), tag=tag, align_bytes=ALIGN)
             nc.vector.memset(window[:], 0.0)
             windows.append(window)
 
         new_window("window0")
 
-        nc.scalar.dma_start(w4_sc_raw[ROWS_AT:P, :], w4_scales.rearrange("a q c -> (a q) c").bitcast(I32))
+        loaded_rows = slice(ROWS_AT, ROWS_AT + ROWS_STEP * PASSES * BLOCKS, ROWS_STEP)
         nc.scalar.activation(one[:], seed[:], ACT.Sqrt)
+        nc.scalar.dma_start(w4_sc_raw[loaded_rows, :], w4_scales.rearrange("a q c -> (a q) c").bitcast(I32))
 
         def load_w1(raw, a, columns):
             nc.sync.dma_start(raw, w1[a * K_PASS : (a + 1) * K_PASS, columns].rearrange("(p i) c -> p i c", i=PACK))
-            return raw.rearrange("p i (q t m) -> p t q m i", t=PACK, m=RUN)
+            return raw.rearrange("p i (g t l) -> p t g i l", t=PACK, l=LINE)
 
         def load_table(a, words):
             nc.sync.dma_start(words[:], tab_words[a].rearrange("p t i -> p (t i)").bitcast(I32))
             return words[:].bitcast(U32)
 
-        nc.sync.dma_start(tab_sc[ROWS_AT:P, :], tab_scales.rearrange("a q t -> (a q) t").bitcast(I32))
         nc.sync.dma_start(idx[:], offs)
+        nc.sync.dma_start(idx2[:], offs2)
+        first_raw = keep.tile([P, PACK, H], F32, name="w1_raw0", align_bytes=ALIGN)
+        w1_first = load_w1(first_raw[:], 0, slice(0, H))
+        nc.sync.dma_start(tab_sc[loaded_rows, :], tab_scales.rearrange("a q t -> (a q) t").bitcast(I32))
+        first_words = table.tile([P, T], I32, name="tab0", offset=TABLE_AT, align_bytes=ALIGN)
+        tab_first = load_table(0, first_words)
+
+        def pick_scales(j0, at):
+            picked = staged.tile([P, HALF // WORD], I32, name="picked%d" % j0, offset=at, align_bytes=ALIGN)
+            entries = idx[:, j0 // LIST_ROWS : (j0 + HALF) // LIST_ROWS]
+            nc.vector.tensor_copy(picked[:].bitcast(U8), tab_sc[:].bitcast(U8).indirect(entries))
+            return picked
+
+        picked_lower = pick_scales(0, HALF - ALIGN)
+        rows = keep.tile([P, (H + HALF) // WORD], I32, name="rows", align_bytes=ALIGN)
+        nc.vector.tensor_copy(
+            rows[:, 0 : H // WORD].rearrange("p (t g) -> p t g", t=PACK),
+            w4_sc_raw[:].rearrange("p (g t) -> p t g", t=PACK),
+        )
+        nc.vector.tensor_copy(rows[:, H // WORD :], picked_lower[:])
+        picked_upper = pick_scales(HALF, 0)
         w4_raw = keep.tile([P, PASSES, H // 2], I32, name="w4_raw", tag="w4_raw", align_bytes=ALIGN)
         nc.sync.dma_start(w4_raw[:], w4_words.rearrange("a p c -> p a c").bitcast(I32))
-        first_words = keep.tile([P, T], I32, name="tab0", tag="first_table", align_bytes=ALIGN)
-        tab_first = load_table(0, first_words)
-        nc.sync.dma_start(idx2[:], offs2)
-        first_raw = staged.tile([P, PACK, H], F32, name="w1_raw0", offset=0, align_bytes=ALIGN)
-        w1_first = load_w1(first_raw[:], 0, slice(0, H))
 
-        picked_sc = keep.tile([P, S // WORD], I32, name="picked_sc", tag="second_table", align_bytes=ALIGN)
-        nc.vector.tensor_copy(picked_sc[:].bitcast(U8), tab_sc[:].bitcast(U8).indirect(idx[:]))
-        rows = keep.tile([P, (S + H) // WORD], I32, name="rows", align_bytes=ALIGN)
-        nc.vector.tensor_copy(
-            rows[ROWS_AT:P, 0 : H // WORD].rearrange("p (t q w) -> p t q w", t=PACK, w=RUN // WORD),
-            w4_sc_raw[ROWS_AT:P, :].rearrange("p (q t w) -> p t q w", t=PACK, w=RUN // WORD),
-        )
-        nc.vector.tensor_copy(rows[ROWS_AT:P, H // WORD :], picked_sc[ROWS_AT:P, :])
-
-        def move_scale_rows(a, plane, first, last):
-            start = ROWS_AT + BLOCKS * a
+        def move_scale_rows(a, plane, source):
+            start = ROWS_AT + ROWS_STEP * BLOCKS * a
             for r in range(QUAD_ROWS):
-                source = rows[start + r : start + BLOCKS : QUAD_ROWS, first // WORD : last // WORD]
-                nc.sync.dma_start(plane[r:P:QUAD, :], source)
+                of_row = slice(start + ROWS_STEP * r, start + ROWS_STEP * BLOCKS, ROWS_STEP * QUAD_ROWS)
+                nc.sync.dma_start(plane[r:P:QUAD, :], source[of_row, :])
 
         plane_first = planes[:, 0 : (H + HALF) // WORD]
         plane_second = planes[:, (H + HALF) // WORD :]
-        move_scale_rows(0, plane_first, 0, H + HALF)
-        second_words = keep.tile([P, T], I32, name="tab1", tag="second_table", align_bytes=ALIGN)
+        move_scale_rows(0, plane_first, rows)
+        second_words = staged.tile([P, T], I32, name="tab1", offset=S - 2 * ALIGN, align_bytes=ALIGN)
         tab_second = load_table(1, second_words)
-        move_scale_rows(1, plane_second, 0, H + HALF)
+        move_scale_rows(1, plane_second, rows)
 
         w4_q = keep.tile([P, PASSES, H // 2], I32, name="w4_q", align_bytes=ALIGN)
         for a in range(PASSES):
             nc.vector.tensor_copy(
-                w4_q[:, a, :].rearrange("p (t q w) -> p t q w", t=PACK, w=RUN // 2),
-                w4_raw[:, a, :].rearrange("p (q t w) -> p t q w", t=PACK, w=RUN // 2),
+                w4_q[:, a, :].rearrange("p (t g w) -> p t g w", t=PACK, w=LINE // 2),
+                w4_raw[:, a, :].rearrange("p (g t w) -> p t g w", t=PACK, w=LINE // 2),
             )
 
         v_q = {}
@@ -127,8 +140,8 @@ def tile_list_replay_huber_novelty_kernel(
             nc.vector.tensor_copy(v_q[a, j0][:], table.indirect(idx[:, j0 // LIST_ROWS : (j0 + HALF) // LIST_ROWS]))
 
         pick_words(0, 0, tab_first, "v_q00")
-        pick_words(0, HALF, tab_first, "v_q01")
-        second_raw = keep.tile([P, PACK * H], F32, name="w1_raw1", tag="first_table", align_bytes=ALIGN)
+        pick_words(0, HALF, tab_first, "w4_raw")
+        second_raw = keep.tile([P, PACK * H], F32, name="w1_raw1", tag="tab_sc", align_bytes=ALIGN)
         w1_second = []
         for half in range(2):
             raw = second_raw[:, half * PACK * H // 2 : (half + 1) * PACK * H // 2].rearrange("p (i c) -> p i c", i=PACK)
@@ -143,7 +156,7 @@ def tile_list_replay_huber_novelty_kernel(
                 for t in range(PACK)
             ]
             for t in range(PACK):
-                grouped = rounded[t][:].rearrange("p (q m i) -> p q m i", m=RUN, i=PACK)
+                grouped = rounded[t][:].rearrange("p (g l i) -> p g i l", l=LINE, i=PACK)
                 if t in on_scalar:
                     nc.scalar.activation(grouped, raw[:, t], ACT.Copy, scale=-1.0)
                 else:
@@ -154,28 +167,28 @@ def tile_list_replay_huber_novelty_kernel(
                     out=w1_q[:, a, features].bitcast(FP8X4), scales=w1_sc[:, a, features], in_=rounded[t][:]
                 )
 
-        new_window("w4_raw")
-        quantise_w1(0, w1_first, 0, P, "w1_bf0", (1, 3))
+        quantise_w1(0, w1_first, 0, P, "w1_bf0", (0, 1, 2, 3))
         new_window("w1_bf0_3")
+        new_window(None)
         windows.append(windows[0])
 
-        w2_rows = w2.rearrange("(q t m) n -> t q m n", t=PACK, m=RUN)
+        w2_rows = w2.rearrange("(g t l) n -> t g l n", t=PACK, l=LINE)
         early = EARLY_TILES * P
-        later = staged.tile([P, PACK * early + S], F32, name="w2_wgo", offset=S, align_bytes=ALIGN)
+        later = table.tile([P, PACK * early + S], F32, name="w2_wgo", offset=9 * S, align_bytes=ALIGN)
         w2_early = later[:, 0 : PACK * early].rearrange("p (t n) -> p t n", t=PACK)
         wgo_sb = later[:, PACK * early :]
         for t in range(PACK):
             nc.sync.dma_start(w2_early[:, t, :], w2_rows[t][:, :, 0:early])
         nc.sync.dma_start(wgo_sb, wgo)
-        plane_late = staged.tile([P, S // WORD], I32, name="plane_late", offset=0, align_bytes=ALIGN)
+        plane_late = table.tile([P, S // WORD], I32, name="plane_late", offset=8 * S, align_bytes=ALIGN)
         nc.vector.memset(plane_late[:], 0)
         for a in range(PASSES):
-            move_scale_rows(a, plane_late[:, a * HALF // WORD : (a + 1) * HALF // WORD], H + HALF, H + S)
+            move_scale_rows(a, plane_late[:, a * HALF // WORD : (a + 1) * HALF // WORD], picked_upper)
 
         pick_words(1, 0, tab_second, "v_q10")
         quantise_w1(1, w1_second[0], 0, P // 2, "w1_bf1", (1, 3))
         quantise_w1(1, w1_second[1], P // 2, P // 2, "w1_bf2", (3,))
-        pick_words(1, HALF, tab_second, "w1_bf2_3")
+        pick_words(1, HALF, tab_second, "w1_bf2_2")
         w4_scale_bytes = [plane.bitcast(U8)[:, 0:H] for plane in (plane_first, plane_second)]
 
         def v_scale_bytes(a, j0):
@@ -186,8 +199,7 @@ def tile_list_replay_huber_novelty_kernel(
         w2_q = keep.tile([P, N], U32, name="w2_q", align_bytes=ALIGN)
         w2_sc = keep.tile([P, N], U8, name="w2_sc", align_bytes=ALIGN)
 
-        def quantise_w2(first, width, raw, on_scalar):
-            heads = slice(first, first + width)
+        def round_w2(first, width, raw, on_scalar):
             rounded = keep.tile([P, width, PACK], BF16, name="w2_bf%d" % first, align_bytes=ALIGN)
             if on_scalar:
                 nc.scalar.activation(rounded[:], raw.rearrange("p t n -> p n t"), ACT.Copy)
@@ -195,11 +207,15 @@ def tile_list_replay_huber_novelty_kernel(
                 nc.vector.tensor_copy(
                     rounded[:].rearrange("p (c n) t -> p c t n", n=LINE), raw.rearrange("p t (c n) -> p c t n", n=LINE)
                 )
+            return rounded
+
+        def quantise_w2(first, width, rounded):
+            heads = slice(first, first + width)
             nc.vector.quantize_mx(
                 out=w2_q[:, heads].bitcast(FP8X4), scales=w2_sc[:, heads], in_=rounded[:].rearrange("p n t -> p (n t)")
             )
 
-        quantise_w2(0, early, w2_early, False)
+        w2_rounded = round_w2(0, early, w2_early, False)
 
         h_bf = [
             keep.tile([P, CHUNK, PACK], BF16, name="h_bf%d" % c, tag="h_bf%d" % c, align_bytes=ALIGN)
@@ -271,6 +287,8 @@ def tile_list_replay_huber_novelty_kernel(
         for j0 in range(0, CHUNK, COLS):
             square_differences(j0)
             quantise_h(j0, COLS)
+            if j0 == 0:
+                quantise_w2(0, early, w2_rounded)
         w2_late = keep.tile([P, PACK, N - early], F32, name="w2_late", tag="h_bf0", align_bytes=ALIGN)
         for t in range(PACK):
             nc.sync.dma_start(w2_late[:, t, :], w2_rows[t][:, :, early:N])
@@ -290,7 +308,7 @@ def tile_list_replay_huber_novelty_kernel(
             for n in range(1, EARLY_TILES):
                 place(n, j0, CHUNK)
 
-        quantise_w2(early, N - early, w2_late[:], True)
+        quantise_w2(early, N - early, round_w2(early, N - early, w2_late[:], True))
         for n in range(EARLY_TILES, N // P):
             for j0 in range(0, S, HALF):
                 score(n, j0, HALF, 2 + 2 * (j0 // HALF))

@@ -35,6 +35,7 @@ HALF = 512
 AHEAD = (3, 2, 2, 0)
 EARLY_TILES = 2
 TABLE_AT = 8128
+KB = 1024
 ALIGN = 64
 
 GROUP = ((False, 0), (True, 0), (False, 1), (True, 1))
@@ -49,6 +50,7 @@ def tile_list_replay_huber_novelty_kernel(
         keep = ctx.enter_context(tc.tile_pool(name="keep", bufs=1))
         table = ctx.enter_context(tc.tile_pool(name="table", bufs=1))
         staged = ctx.enter_context(tc.tile_pool(name="staged", bufs=1))
+        chain = ctx.enter_context(tc.tile_pool(name="chain", bufs=1))
         banks = ctx.enter_context(tc.psum_pool(name="banks", bufs=1))
 
         idx = lists.tile([P, S // LIST_ROWS], U16, name="idx")
@@ -59,10 +61,13 @@ def tile_list_replay_huber_novelty_kernel(
         planes = keep.tile([P, PASSES * (H + HALF) // WORD], I32, name="planes", align_bytes=ALIGN)
         seed = table.tile([P, 1], F32, name="seed", offset=TABLE_AT, align_bytes=ALIGN)
         one = keep.tile([P, 1], F32, name="one")
+        first_ones = chain.tile([P, 2 * ALIGN // WORD], F32, name="first_ones", offset=KB - ALIGN, align_bytes=ALIGN)
+        first_one = first_ones[:, 0:1]
         nc.vector.memset(seed[:], 1.0)
         nc.vector.memset(tab_sc[:], 0)
         nc.vector.memset(w4_sc_raw[:], 0)
         nc.vector.memset(planes[:], 0)
+        nc.vector.memset(one[:], 1.0)
 
         windows = []
 
@@ -77,7 +82,7 @@ def tile_list_replay_huber_novelty_kernel(
         new_window("window0")
 
         loaded_rows = slice(ROWS_AT, ROWS_AT + ROWS_STEP * PASSES * BLOCKS, ROWS_STEP)
-        nc.scalar.activation(one[:], seed[:], ACT.Sqrt)
+        nc.scalar.activation(first_one, seed[:], ACT.Sqrt)
         nc.scalar.dma_start(w4_sc_raw[loaded_rows, :], w4_scales.rearrange("a q c -> (a q) c").bitcast(I32))
 
         def load_w1(raw, a, columns):
@@ -135,9 +140,14 @@ def tile_list_replay_huber_novelty_kernel(
 
         v_q = {}
 
-        def pick_words(a, j0, table, tag):
-            v_q[a, j0] = keep.tile([P, HALF], U32, name="v_q%d_%d" % (a, j0), tag=tag, align_bytes=ALIGN)
-            nc.vector.tensor_copy(v_q[a, j0][:], table.indirect(idx[:, j0 // LIST_ROWS : (j0 + HALF) // LIST_ROWS]))
+        def pick_words(a, j0, table, tag, width=HALF):
+            if tag is None:
+                words = chain.tile([P, width], U32, name="v_q%d_%d" % (a, j0), offset=7 * KB // 2, align_bytes=ALIGN)
+            else:
+                words = keep.tile([P, width], U32, name="v_q%d_%d" % (a, j0), tag=tag, align_bytes=ALIGN)
+            nc.vector.tensor_copy(words[:], table.indirect(idx[:, j0 // LIST_ROWS : (j0 + width) // LIST_ROWS]))
+            for j in range(j0, j0 + width, COLS):
+                v_q[a, j] = words[:, j - j0 : j - j0 + COLS]
 
         pick_words(0, 0, tab_first, "v_q00")
         pick_words(0, HALF, tab_first, "w4_raw")
@@ -174,12 +184,11 @@ def tile_list_replay_huber_novelty_kernel(
 
         w2_rows = w2.rearrange("(g t l) n -> t g l n", t=PACK, l=LINE)
         early = EARLY_TILES * P
-        later = table.tile([P, PACK * early + S], F32, name="w2_wgo", offset=9 * S, align_bytes=ALIGN)
-        w2_early = later[:, 0 : PACK * early].rearrange("p (t n) -> p t n", t=PACK)
-        wgo_sb = later[:, PACK * early :]
+        w2_early = table.tile([P, PACK, early], F32, name="w2_early", offset=9 * KB, align_bytes=ALIGN)
+        wgo_sb = table.tile([P, S], F32, name="wgo_sb", offset=13 * KB, align_bytes=ALIGN)
         for t in range(PACK):
             nc.sync.dma_start(w2_early[:, t, :], w2_rows[t][:, :, 0:early])
-        nc.sync.dma_start(wgo_sb, wgo)
+        nc.sync.dma_start(wgo_sb[:], wgo)
         plane_late = table.tile([P, S // WORD], I32, name="plane_late", offset=8 * S, align_bytes=ALIGN)
         nc.vector.memset(plane_late[:], 0)
         for a in range(PASSES):
@@ -188,7 +197,7 @@ def tile_list_replay_huber_novelty_kernel(
         pick_words(1, 0, tab_second, "v_q10")
         quantise_w1(1, w1_second[0], 0, P // 2, "w1_bf1", (1, 3))
         quantise_w1(1, w1_second[1], P // 2, P // 2, "w1_bf2", (3,))
-        pick_words(1, HALF, tab_second, "w1_bf2_2")
+        pick_words(1, HALF, tab_second, "w1_bf2_2", CHUNK)
         w4_scale_bytes = [plane.bitcast(U8)[:, 0:H] for plane in (plane_first, plane_second)]
 
         def v_scale_bytes(a, j0):
@@ -215,14 +224,21 @@ def tile_list_replay_huber_novelty_kernel(
                 out=w2_q[:, heads].bitcast(FP8X4), scales=w2_sc[:, heads], in_=rounded[:].rearrange("p n t -> p (n t)")
             )
 
-        w2_rounded = round_w2(0, early, w2_early, False)
+        w2_rounded = round_w2(0, early, w2_early[:], False)
 
-        h_bf = [
-            keep.tile([P, CHUNK, PACK], BF16, name="h_bf%d" % c, tag="h_bf%d" % c, align_bytes=ALIGN)
-            for c in range(S // CHUNK)
-        ]
+        h_bf = {}
+        for j0 in range(0, S, COLS):
+            if j0 < HALF or j0 % CHUNK == 0:
+                width = COLS if j0 < HALF else CHUNK
+                if j0 in (COLS, HALF - COLS):
+                    at = 4 * KB if j0 == COLS else 0
+                    tile = chain.tile([P, width, PACK], BF16, name="h_bf%d" % j0, offset=at, align_bytes=ALIGN)
+                else:
+                    tile = keep.tile([P, width, PACK], BF16, name="h_bf%d" % j0, tag="h_bf%d" % j0, align_bytes=ALIGN)
+                first = j0
+            h_bf[j0] = (tile, j0 - first)
         h_q = keep.tile([P, S], U32, name="h_q", align_bytes=ALIGN)
-        h_sc = keep.tile([P, S], U8, name="h_sc", align_bytes=ALIGN)
+        h_sc = table.tile([P, S], U8, name="h_sc", offset=9 * KB, align_bytes=ALIGN)
 
         def square_differences(j0):
             bank = j0 // COLS
@@ -242,24 +258,28 @@ def tile_list_replay_huber_novelty_kernel(
                         diff[:, t, :],
                         lhsT=codes,
                         lhsT_scale=scales,
-                        rhs=v_q[a, j0 - j0 % HALF][:, j0 % HALF : j0 % HALF + COLS].bitcast(FP8X4),
+                        rhs=v_q[a, j0].bitcast(FP8X4),
                         rhs_scale=v_scale_bytes(a, j0),
                         start=(step == 0 and count == 0),
                         stop=(step == len(GROUP) - 1 and count == PACK - 1),
                     )
-            nc.scalar.activation(
-                h_bf[j0 // CHUNK][:, j0 % CHUNK : j0 % CHUNK + COLS, :], diff[:].rearrange("p t j -> p j t"), ACT.Square
-            )
+            tile, first = h_bf[j0]
+            nc.scalar.activation(tile[:, first : first + COLS, :], diff[:].rearrange("p t j -> p j t"), ACT.Square)
 
         def quantise_h(j0, width):
             cols = slice(j0, j0 + width)
             nc.vector.quantize_mx(
                 out=h_q[:, cols].bitcast(FP8X4),
                 scales=h_sc[:, cols],
-                in_=h_bf[j0 // CHUNK][:, j0 % CHUNK : j0 % CHUNK + width, :].rearrange("p j t -> p (j t)"),
+                in_=h_bf[j0][0][:].rearrange("p j t -> p (j t)"),
             )
 
         ys = [keep.tile([P, S], F32, name="y%d" % n, align_bytes=ALIGN) for n in range(N // P)]
+
+        second_y = chain.tile([P, CHUNK], F32, name="second_y", offset=KB, align_bytes=ALIGN)
+
+        def y_of(n, j0, width):
+            return second_y[:] if (n, j0) == (1, 0) else ys[n][:, j0 : j0 + width]
 
         def score(n, j0, width, bank):
             cols = slice(j0, j0 + width)
@@ -274,12 +294,12 @@ def tile_list_replay_huber_novelty_kernel(
                 start=True,
                 stop=True,
             )
-            nc.scalar.activation(ys[n][:, cols], x[:], ACT.Sqrt, bias=one[:])
+            nc.scalar.activation(y_of(n, j0, width), x[:], ACT.Sqrt, bias=first_one if n == 0 and j0 < CHUNK else one[:])
 
         def place(n, j0, width):
             places = idx2[:, j0 // LIST_ROWS : (j0 + width) // LIST_ROWS]
             nc.vector.tensor_tensor(
-                windows[n][:].indirect(places), ys[n][:, j0 : j0 + width], wgo_sb[:, j0 : j0 + width], MULT
+                windows[n][:].indirect(places), y_of(n, j0, width), wgo_sb[:, j0 : j0 + width], MULT
             )
             if j0 + width == S:
                 nc.sync.dma_start(out[n * P : (n + 1) * P, :], windows[n][:])
@@ -289,7 +309,8 @@ def tile_list_replay_huber_novelty_kernel(
             quantise_h(j0, COLS)
             if j0 == 0:
                 quantise_w2(0, early, w2_rounded)
-        w2_late = keep.tile([P, PACK, N - early], F32, name="w2_late", tag="h_bf0", align_bytes=ALIGN)
+        pick_words(1, S - CHUNK, tab_second, None, CHUNK)
+        w2_late = chain.tile([P, PACK, N - early], F32, name="w2_late", offset=9 * KB // 2, align_bytes=ALIGN)
         for t in range(PACK):
             nc.sync.dma_start(w2_late[:, t, :], w2_rows[t][:, :, early:N])
         score(0, 0, COLS, 0)
@@ -301,10 +322,12 @@ def tile_list_replay_huber_novelty_kernel(
                 square_differences(following + COLS)
             for n in range(EARLY_TILES):
                 if n > 0 or j0 > 0:
-                    score(n, j0, CHUNK, (following // COLS + n) % BANKS)
+                    score(n, j0, CHUNK, 2 if j0 == 0 else (following // COLS + n) % BANKS)
             place(0, j0, CHUNK)
             if following < S:
-                quantise_h(following, CHUNK)
+                step = COLS if following < HALF else CHUNK
+                for j in range(following, following + CHUNK, step):
+                    quantise_h(j, step)
             for n in range(1, EARLY_TILES):
                 place(n, j0, CHUNK)
 

@@ -32,7 +32,7 @@ LIST_ROWS = 16
 COLS = 128
 CHUNK = 256
 HALF = 512
-AHEAD = (3, 2, 2, 0)
+AHEAD = (3, 3, 2, 0)
 EARLY_TILES = 2
 TABLE_AT = 8128
 KB = 1024

@@ -32,13 +32,19 @@ LIST_ROWS = 16
 COLS = 128
 CHUNK = 256
 HALF = 512
-AHEAD = (3, 3, 2, 0)
 EARLY_TILES = 2
-TABLE_AT = 8128
 KB = 1024
 ALIGN = 64
+TABLE_AT = 8 * KB - ALIGN
+SECOND_AT = TABLE_AT + WORD * T
 
-GROUP = ((False, 0), (True, 0), (False, 1), (True, 1))
+W4_0, W4_1, W1_0, W1_1 = (False, 0), (False, 1), (True, 0), (True, 1)
+STEPS = (
+    (W4_0, W4_1, W1_0, W1_1),
+    (W4_0, W4_1, W1_1, W1_0),
+    (W4_0, W1_0, W1_1, W4_1),
+    (W1_1, W4_0, W1_0, W4_1),
+)
 
 
 def tile_list_replay_huber_novelty_kernel(
@@ -50,56 +56,52 @@ def tile_list_replay_huber_novelty_kernel(
         keep = ctx.enter_context(tc.tile_pool(name="keep", bufs=1))
         table = ctx.enter_context(tc.tile_pool(name="table", bufs=1))
         staged = ctx.enter_context(tc.tile_pool(name="staged", bufs=1))
+        scale = ctx.enter_context(tc.tile_pool(name="scale", bufs=1))
+        first_out = ctx.enter_context(tc.tile_pool(name="first_out", bufs=1))
+        second_out = ctx.enter_context(tc.tile_pool(name="second_out", bufs=1))
         chain = ctx.enter_context(tc.tile_pool(name="chain", bufs=1))
         banks = ctx.enter_context(tc.psum_pool(name="banks", bufs=1))
 
         idx = lists.tile([P, S // LIST_ROWS], U16, name="idx")
         idx2 = lists.tile([P, S // LIST_ROWS], U16, name="idx2")
 
-        tab_sc = keep.tile([P, T // WORD], I32, name="tab_sc", tag="tab_sc", align_bytes=ALIGN)
-        w4_sc_raw = keep.tile([P, H // WORD], I32, name="w4_sc_raw", tag="w4_raw", align_bytes=ALIGN)
+        seeds = table.tile([P, 2 * ALIGN // WORD], F32, name="seeds", offset=SECOND_AT - ALIGN, align_bytes=ALIGN)
+        seed = seeds[:, 0:1]
+        tab_sc = scale.tile([P, T // WORD], I32, name="tab_sc", offset=0, align_bytes=ALIGN)
+        w4_sc_raw = keep.tile([P, H // WORD], I32, name="w4_sc_raw", align_bytes=ALIGN)
         planes = keep.tile([P, PASSES * (H + HALF) // WORD], I32, name="planes", align_bytes=ALIGN)
-        seed = table.tile([P, 1], F32, name="seed", offset=TABLE_AT, align_bytes=ALIGN)
         one = keep.tile([P, 1], F32, name="one")
         first_ones = chain.tile([P, 2 * ALIGN // WORD], F32, name="first_ones", offset=KB - ALIGN, align_bytes=ALIGN)
         first_one = first_ones[:, 0:1]
-        nc.vector.memset(seed[:], 1.0)
+        nc.gpsimd.memset(w4_sc_raw[:], 0)
+        nc.gpsimd.memset(seed, 1.0)
         nc.vector.memset(tab_sc[:], 0)
-        nc.vector.memset(w4_sc_raw[:], 0)
+        nc.vector.tensor_copy(one[:], seed)
         nc.vector.memset(planes[:], 0)
-        nc.vector.memset(one[:], 1.0)
-
-        windows = []
-
-        def new_window(tag):
-            if tag is None:
-                window = table.tile([P, T2], F32, name="window2", offset=0, align_bytes=ALIGN)
-            else:
-                window = keep.tile([P, T2], F32, name="window%d" % len(windows), tag=tag, align_bytes=ALIGN)
-            nc.vector.memset(window[:], 0.0)
-            windows.append(window)
-
-        new_window("window0")
 
         loaded_rows = slice(ROWS_AT, ROWS_AT + ROWS_STEP * PASSES * BLOCKS, ROWS_STEP)
-        nc.scalar.activation(first_one, seed[:], ACT.Sqrt)
-        nc.scalar.dma_start(w4_sc_raw[loaded_rows, :], w4_scales.rearrange("a q c -> (a q) c").bitcast(I32))
+        nc.scalar.activation(first_one, one[:], ACT.Sqrt)
 
-        def load_w1(raw, a, columns):
-            nc.sync.dma_start(raw, w1[a * K_PASS : (a + 1) * K_PASS, columns].rearrange("(p i) c -> p i c", i=PACK))
-            return raw.rearrange("p i (g t l) -> p t g i l", t=PACK, l=LINE)
+        def load_w1(raw, a, first, width):
+            rows_of = raw.rearrange("p (i c) -> p i c", i=PACK)
+            source = w1[a * K_PASS : (a + 1) * K_PASS, first : first + width]
+            nc.sync.dma_start(rows_of, source.rearrange("(p i) c -> p i c", i=PACK))
+            return rows_of.rearrange("p i (g t l) -> p t g i l", t=PACK, l=LINE)
 
         def load_table(a, words):
             nc.sync.dma_start(words[:], tab_words[a].rearrange("p t i -> p (t i)").bitcast(I32))
             return words[:].bitcast(U32)
 
+        w4_raw = keep.tile([P, PASSES, H // 2], I32, name="w4_raw", align_bytes=ALIGN)
+        nc.sync.dma_start(w4_raw[:], w4_words.rearrange("a p c -> p a c").bitcast(I32))
         nc.sync.dma_start(idx[:], offs)
         nc.sync.dma_start(idx2[:], offs2)
-        first_raw = keep.tile([P, PACK, H], F32, name="w1_raw0", align_bytes=ALIGN)
-        w1_first = load_w1(first_raw[:], 0, slice(0, H))
+        nc.sync.dma_start(w4_sc_raw[loaded_rows, :], w4_scales.rearrange("a q c -> (a q) c").bitcast(I32))
         nc.sync.dma_start(tab_sc[loaded_rows, :], tab_scales.rearrange("a q t -> (a q) t").bitcast(I32))
         first_words = table.tile([P, T], I32, name="tab0", offset=TABLE_AT, align_bytes=ALIGN)
         tab_first = load_table(0, first_words)
+        second_words = table.tile([P, T], I32, name="tab1", offset=SECOND_AT, align_bytes=ALIGN)
+        tab_second = load_table(1, second_words)
 
         def pick_scales(j0, at):
             picked = staged.tile([P, HALF // WORD], I32, name="picked%d" % j0, offset=at, align_bytes=ALIGN)
@@ -115,8 +117,6 @@ def tile_list_replay_huber_novelty_kernel(
         )
         nc.vector.tensor_copy(rows[:, H // WORD :], picked_lower[:])
         picked_upper = pick_scales(HALF, 0)
-        w4_raw = keep.tile([P, PASSES, H // 2], I32, name="w4_raw", tag="w4_raw", align_bytes=ALIGN)
-        nc.sync.dma_start(w4_raw[:], w4_words.rearrange("a p c -> p a c").bitcast(I32))
 
         def move_scale_rows(a, plane, source):
             start = ROWS_AT + ROWS_STEP * BLOCKS * a
@@ -127,42 +127,18 @@ def tile_list_replay_huber_novelty_kernel(
         plane_first = planes[:, 0 : (H + HALF) // WORD]
         plane_second = planes[:, (H + HALF) // WORD :]
         move_scale_rows(0, plane_first, rows)
-        second_words = staged.tile([P, T], I32, name="tab1", offset=S - 2 * ALIGN, align_bytes=ALIGN)
-        tab_second = load_table(1, second_words)
+        late_raw = staged.tile([P, PASSES * PACK * H], F32, name="w1_raw", offset=S - 2 * ALIGN, align_bytes=ALIGN)
+        w1_0 = load_w1(late_raw[:, 0 : 4 * H], 0, 0, H)
         move_scale_rows(1, plane_second, rows)
-
-        w4_q = keep.tile([P, PASSES, H // 2], I32, name="w4_q", align_bytes=ALIGN)
-        for a in range(PASSES):
-            nc.vector.tensor_copy(
-                w4_q[:, a, :].rearrange("p (t g w) -> p t g w", t=PACK, w=LINE // 2),
-                w4_raw[:, a, :].rearrange("p (g t w) -> p t g w", t=PACK, w=LINE // 2),
-            )
-
-        v_q = {}
-
-        def pick_words(a, j0, table, tag, width=HALF):
-            if tag is None:
-                words = chain.tile([P, width], U32, name="v_q%d_%d" % (a, j0), offset=7 * KB // 2, align_bytes=ALIGN)
-            else:
-                words = keep.tile([P, width], U32, name="v_q%d_%d" % (a, j0), tag=tag, align_bytes=ALIGN)
-            nc.vector.tensor_copy(words[:], table.indirect(idx[:, j0 // LIST_ROWS : (j0 + width) // LIST_ROWS]))
-            for j in range(j0, j0 + width, COLS):
-                v_q[a, j] = words[:, j - j0 : j - j0 + COLS]
-
-        pick_words(0, 0, tab_first, "v_q00")
-        pick_words(0, HALF, tab_first, "w4_raw")
-        second_raw = keep.tile([P, PACK * H], F32, name="w1_raw1", tag="tab_sc", align_bytes=ALIGN)
-        w1_second = []
-        for half in range(2):
-            raw = second_raw[:, half * PACK * H // 2 : (half + 1) * PACK * H // 2].rearrange("p (i c) -> p i c", i=PACK)
-            w1_second.append(load_w1(raw, 1, slice(half * H // 2, (half + 1) * H // 2)))
+        w1_10 = load_w1(late_raw[:, 4 * H : 6 * H], 1, 0, H // 2)
+        w1_11 = load_w1(late_raw[:, 6 * H : 8 * H], 1, H // 2, H // 2)
 
         w1_q = keep.tile([P, PASSES, H], U32, name="w1_q", align_bytes=ALIGN)
         w1_sc = keep.tile([P, PASSES, H], U8, name="w1_sc", align_bytes=ALIGN)
 
-        def quantise_w1(a, raw, first, width, tag, on_scalar):
+        def quantise_w1(a, raw, first, width, on_scalar):
             rounded = [
-                keep.tile([P, width * PACK], BF16, name="%s_%d" % (tag, t), tag="%s_%d" % (tag, t), align_bytes=ALIGN)
+                keep.tile([P, width * PACK], BF16, name="w1_bf%d%d_%d" % (a, first, t), align_bytes=ALIGN)
                 for t in range(PACK)
             ]
             for t in range(PACK):
@@ -177,9 +153,33 @@ def tile_list_replay_huber_novelty_kernel(
                     out=w1_q[:, a, features].bitcast(FP8X4), scales=w1_sc[:, a, features], in_=rounded[t][:]
                 )
 
-        quantise_w1(0, w1_first, 0, P, "w1_bf0", (0, 1, 2, 3))
-        new_window("w1_bf0_3")
-        new_window(None)
+        windows = []
+
+        def new_window(pool):
+            window = pool.tile([P, T2], F32, name="window%d" % len(windows), offset=0, align_bytes=ALIGN)
+            nc.vector.memset(window[:], 0.0)
+            windows.append(window)
+
+        w4_q = keep.tile([P, PASSES, H // 2], I32, name="w4_q", align_bytes=ALIGN)
+        for a in range(PASSES):
+            nc.vector.tensor_copy(
+                w4_q[:, a, :].rearrange("p (t g w) -> p t g w", t=PACK, w=LINE // 2),
+                w4_raw[:, a, :].rearrange("p (g t w) -> p t g w", t=PACK, w=LINE // 2),
+            )
+        new_window(first_out)
+        new_window(second_out)
+        new_window(scale)
+
+        v_q = {}
+
+        def pick_words(a, j0, words_of, tag, width):
+            words = keep.tile([P, width], U32, name="v_q%d_%d" % (a, j0), tag=tag, align_bytes=ALIGN)
+            nc.vector.tensor_copy(words[:], words_of.indirect(idx[:, j0 // LIST_ROWS : (j0 + width) // LIST_ROWS]))
+            for j in range(j0, j0 + width, COLS):
+                v_q[a, j] = words[:, j - j0 : j - j0 + COLS]
+
+        pick_words(0, 0, tab_first, "v_q00", HALF)
+        pick_words(0, HALF, tab_first, "v_q02", HALF)
         windows.append(windows[0])
 
         w2_rows = w2.rearrange("(g t l) n -> t g l n", t=PACK, l=LINE)
@@ -189,15 +189,19 @@ def tile_list_replay_huber_novelty_kernel(
         for t in range(PACK):
             nc.sync.dma_start(w2_early[:, t, :], w2_rows[t][:, :, 0:early])
         nc.sync.dma_start(wgo_sb[:], wgo)
-        plane_late = table.tile([P, S // WORD], I32, name="plane_late", offset=8 * S, align_bytes=ALIGN)
+        plane_late = table.tile([P, S // WORD], I32, name="plane_late", offset=8 * KB, align_bytes=ALIGN)
         nc.vector.memset(plane_late[:], 0)
         for a in range(PASSES):
             move_scale_rows(a, plane_late[:, a * HALF // WORD : (a + 1) * HALF // WORD], picked_upper)
 
-        pick_words(1, 0, tab_second, "v_q10")
-        quantise_w1(1, w1_second[0], 0, P // 2, "w1_bf1", (1, 3))
-        quantise_w1(1, w1_second[1], P // 2, P // 2, "w1_bf2", (3,))
-        pick_words(1, HALF, tab_second, "w1_bf2_2", CHUNK)
+        pick_words(1, 0, tab_second, "v_q10", HALF)
+        pick_words(1, HALF, tab_second, "v_q12", HALF)
+        quantise_w1(0, w1_0, 0, P, (2, 3))
+        quantise_w1(1, w1_10, 0, P // 2, (3,))
+        quantise_w1(1, w1_11, P // 2, P // 2, (3,))
+        w2_late = table.tile([P, PACK, N - early], F32, name="w2_late", offset=SECOND_AT, align_bytes=ALIGN)
+        for t in range(PACK):
+            nc.sync.dma_start(w2_late[:, t, :], w2_rows[t][:, :, early:N])
         w4_scale_bytes = [plane.bitcast(U8)[:, 0:H] for plane in (plane_first, plane_second)]
 
         def v_scale_bytes(a, j0):
@@ -209,19 +213,19 @@ def tile_list_replay_huber_novelty_kernel(
         w2_sc = keep.tile([P, N], U8, name="w2_sc", align_bytes=ALIGN)
 
         def round_w2(first, width, raw, on_scalar):
-            rounded = keep.tile([P, width, PACK], BF16, name="w2_bf%d" % first, align_bytes=ALIGN)
+            tile = keep.tile([P, width, PACK], BF16, name="w2_bf%d" % first, align_bytes=ALIGN)
             if on_scalar:
-                nc.scalar.activation(rounded[:], raw.rearrange("p t n -> p n t"), ACT.Copy)
+                nc.scalar.activation(tile[:], raw.rearrange("p t n -> p n t"), ACT.Copy)
             else:
                 nc.vector.tensor_copy(
-                    rounded[:].rearrange("p (c n) t -> p c t n", n=LINE), raw.rearrange("p t (c n) -> p c t n", n=LINE)
+                    tile[:].rearrange("p (c n) t -> p c t n", n=LINE), raw.rearrange("p t (c n) -> p c t n", n=LINE)
                 )
-            return rounded
+            return tile
 
-        def quantise_w2(first, width, rounded):
+        def quantise_w2(first, width, tile):
             heads = slice(first, first + width)
             nc.vector.quantize_mx(
-                out=w2_q[:, heads].bitcast(FP8X4), scales=w2_sc[:, heads], in_=rounded[:].rearrange("p n t -> p (n t)")
+                out=w2_q[:, heads].bitcast(FP8X4), scales=w2_sc[:, heads], in_=tile[:].rearrange("p n t -> p (n t)")
             )
 
         w2_rounded = round_w2(0, early, w2_early[:], False)
@@ -230,11 +234,10 @@ def tile_list_replay_huber_novelty_kernel(
         for j0 in range(0, S, COLS):
             if j0 < HALF or j0 % CHUNK == 0:
                 width = COLS if j0 < HALF else CHUNK
-                if j0 in (COLS, HALF - COLS):
-                    at = 4 * KB if j0 == COLS else 0
-                    tile = chain.tile([P, width, PACK], BF16, name="h_bf%d" % j0, offset=at, align_bytes=ALIGN)
+                if j0 == HALF - COLS:
+                    tile = chain.tile([P, width, PACK], BF16, name="h_bf%d" % j0, offset=0, align_bytes=ALIGN)
                 else:
-                    tile = keep.tile([P, width, PACK], BF16, name="h_bf%d" % j0, tag="h_bf%d" % j0, align_bytes=ALIGN)
+                    tile = keep.tile([P, width, PACK], BF16, name="h_bf%d" % j0, align_bytes=ALIGN)
                 first = j0
             h_bf[j0] = (tile, j0 - first)
         h_q = keep.tile([P, S], U32, name="h_q", align_bytes=ALIGN)
@@ -243,10 +246,8 @@ def tile_list_replay_huber_novelty_kernel(
         def square_differences(j0):
             bank = j0 // COLS
             diff = banks.tile([P, PACK, COLS], F32, name="diff%d" % bank, tag="bank%d" % bank)
-            before = AHEAD[j0 // CHUNK]
-            order = GROUP[:before] + GROUP[-1:] + GROUP[before:-1]
-            for step, (online, a) in enumerate(order):
-                values = range(PACK) if j0 < CHUNK else reversed(range(PACK))
+            for step, (online, a) in enumerate(STEPS[j0 // CHUNK]):
+                values = range(PACK) if j0 == 0 else reversed(range(PACK))
                 for count, t in enumerate(values):
                     if online:
                         codes = w1_q[:, a, t * P : (t + 1) * P].bitcast(FP8X4)
@@ -261,7 +262,7 @@ def tile_list_replay_huber_novelty_kernel(
                         rhs=v_q[a, j0].bitcast(FP8X4),
                         rhs_scale=v_scale_bytes(a, j0),
                         start=(step == 0 and count == 0),
-                        stop=(step == len(GROUP) - 1 and count == PACK - 1),
+                        stop=(step == 2 * PASSES - 1 and count == PACK - 1),
                     )
             tile, first = h_bf[j0]
             nc.scalar.activation(tile[:, first : first + COLS, :], diff[:].rearrange("p t j -> p j t"), ACT.Square)
@@ -275,7 +276,6 @@ def tile_list_replay_huber_novelty_kernel(
             )
 
         ys = [keep.tile([P, S], F32, name="y%d" % n, align_bytes=ALIGN) for n in range(N // P)]
-
         second_y = chain.tile([P, CHUNK], F32, name="second_y", offset=KB, align_bytes=ALIGN)
 
         def y_of(n, j0, width):
@@ -309,10 +309,6 @@ def tile_list_replay_huber_novelty_kernel(
             quantise_h(j0, COLS)
             if j0 == 0:
                 quantise_w2(0, early, w2_rounded)
-        pick_words(1, S - CHUNK, tab_second, None, CHUNK)
-        w2_late = chain.tile([P, PACK, N - early], F32, name="w2_late", offset=9 * KB // 2, align_bytes=ALIGN)
-        for t in range(PACK):
-            nc.sync.dma_start(w2_late[:, t, :], w2_rows[t][:, :, early:N])
         score(0, 0, COLS, 0)
         score(0, COLS, COLS, 1)
         for j0 in range(0, S, CHUNK):

@@ -73,9 +73,9 @@ def tile_list_replay_huber_novelty_kernel(
         one = keep.tile([P, 1], F32, name="one")
         first_ones = chain.tile([P, 2 * ALIGN // WORD], F32, name="first_ones", offset=KB - ALIGN, align_bytes=ALIGN)
         first_one = first_ones[:, 0:1]
-        nc.gpsimd.memset(w4_sc_raw[:], 0)
-        nc.gpsimd.memset(seed, 1.0)
+        nc.vector.memset(seed, 1.0)
         nc.vector.memset(tab_sc[:], 0)
+        nc.vector.memset(w4_sc_raw[:], 0)
         nc.vector.tensor_copy(one[:], seed)
         nc.vector.memset(planes[:], 0)
 
@@ -96,8 +96,8 @@ def tile_list_replay_huber_novelty_kernel(
         nc.sync.dma_start(w4_raw[:], w4_words.rearrange("a p c -> p a c").bitcast(I32))
         nc.sync.dma_start(idx[:], offs)
         nc.sync.dma_start(idx2[:], offs2)
-        nc.sync.dma_start(w4_sc_raw[loaded_rows, :], w4_scales.rearrange("a q c -> (a q) c").bitcast(I32))
         nc.sync.dma_start(tab_sc[loaded_rows, :], tab_scales.rearrange("a q t -> (a q) t").bitcast(I32))
+        nc.sync.dma_start(w4_sc_raw[loaded_rows, :], w4_scales.rearrange("a q c -> (a q) c").bitcast(I32))
         first_words = table.tile([P, T], I32, name="tab0", offset=TABLE_AT, align_bytes=ALIGN)
         tab_first = load_table(0, first_words)
         second_words = table.tile([P, T], I32, name="tab1", offset=SECOND_AT, align_bytes=ALIGN)

from contextlib import ExitStack

import concourse.mybir as mybir

K, H, N, T, S, T2 = 1024, 512, 512, 4096, 1024, 2048
FLOPS = 2 * K * H * S * 2 + 2 * H * N * S

F32 = mybir.dt.float32
BF16 = mybir.dt.bfloat16
I32 = mybir.dt.int32
U32 = mybir.dt.uint32
U16 = mybir.dt.uint16
U8 = mybir.dt.uint8
FP8X4 = mybir.dt.float8_e4m3fn_x4
FP4X4 = mybir.dt.float4_e2m1fn_x4
ACT = mybir.ActivationFunctionType
MULT = mybir.AluOpType.mult

P = 128
PACK = 4
QUAD = 32
QUAD_ROWS = 4
BLOCKS = 16
ROWS_AT = 32
ROWS_STEP = 2
WORD = 4
BANKS = 8
LINE = 4
K_PASS = P * PACK
PASSES = K // K_PASS
LIST_ROWS = 16
COLS = 128
CHUNK = 256
HALF = 512
EARLY_TILES = 2
KB = 1024
ALIGN = 64
TABLE_AT = 8 * KB - ALIGN
SECOND_AT = TABLE_AT + WORD * T

W4_0, W4_1, W1_0, W1_1 = (False, 0), (False, 1), (True, 0), (True, 1)
STEPS = (
    (W4_0, W4_1, W1_0, W1_1),
    (W4_0, W4_1, W1_1, W1_0),
    (W4_0, W1_0, W1_1, W4_1),
    (W1_1, W4_0, W1_0, W4_1),
)


def tile_list_replay_huber_novelty_kernel(
    tc, tab_words, tab_scales, offs, w1, w4_words, w4_scales, w2, wgo, offs2, out
):
    nc = tc.nc
    with ExitStack() as ctx:
        lists = ctx.enter_context(tc.tile_pool(name="lists", bufs=1))
        keep = ctx.enter_context(tc.tile_pool(name="keep", bufs=1))
        table = ctx.enter_context(tc.tile_pool(name="table", bufs=1))
        staged = ctx.enter_context(tc.tile_pool(name="staged", bufs=1))
        scale = ctx.enter_context(tc.tile_pool(name="scale", bufs=1))
        first_out = ctx.enter_context(tc.tile_pool(name="first_out", bufs=1))
        second_out = ctx.enter_context(tc.tile_pool(name="second_out", bufs=1))
        chain = ctx.enter_context(tc.tile_pool(name="chain", bufs=1))
        banks = ctx.enter_context(tc.psum_pool(name="banks", bufs=1))

        idx = lists.tile([P, S // LIST_ROWS], U16, name="idx")
        idx2 = lists.tile([P, S // LIST_ROWS], U16, name="idx2")

        seeds = table.tile([P, 2 * ALIGN // WORD], F32, name="seeds", offset=SECOND_AT - ALIGN, align_bytes=ALIGN)
        seed = seeds[:, 0:1]
        tab_sc = scale.tile([P, T // WORD], I32, name="tab_sc", offset=0, align_bytes=ALIGN)
        w4_sc_raw = keep.tile([P, H // WORD], I32, name="w4_sc_raw", align_bytes=ALIGN)
        planes = keep.tile([P, PASSES * (H + HALF) // WORD], I32, name="planes", align_bytes=ALIGN)
        one = keep.tile([P, 1], F32, name="one")
        first_ones = chain.tile([P, 2 * ALIGN // WORD], F32, name="first_ones", offset=KB - ALIGN, align_bytes=ALIGN)
        first_one = first_ones[:, 0:1]
        nc.vector.memset(seed, 1.0)
        nc.vector.memset(tab_sc[:], 0)
        nc.vector.memset(w4_sc_raw[:], 0)
        nc.vector.tensor_copy(one[:], seed)
        nc.vector.memset(planes[:], 0)

        loaded_rows = slice(ROWS_AT, ROWS_AT + ROWS_STEP * PASSES * BLOCKS, ROWS_STEP)
        nc.scalar.activation(first_one, one[:], ACT.Sqrt)

        def load_w1(raw, a, first, width):
            rows_of = raw.rearrange("p (i c) -> p i c", i=PACK)
            source = w1[a * K_PASS : (a + 1) * K_PASS, first : first + width]
            nc.sync.dma_start(rows_of, source.rearrange("(p i) c -> p i c", i=PACK))
            return rows_of.rearrange("p i (g t l) -> p t g i l", t=PACK, l=LINE)

        def load_table(a, words):
            nc.sync.dma_start(words[:], tab_words[a].rearrange("p t i -> p (t i)").bitcast(I32))
            return words[:].bitcast(U32)

        w4_raw = keep.tile([P, PASSES, H // 2], I32, name="w4_raw", align_bytes=ALIGN)
        nc.sync.dma_start(w4_raw[:], w4_words.rearrange("a p c -> p a c").bitcast(I32))
        nc.sync.dma_start(idx[:], offs)
        nc.sync.dma_start(idx2[:], offs2)
        nc.sync.dma_start(tab_sc[loaded_rows, :], tab_scales.rearrange("a q t -> (a q) t").bitcast(I32))
        nc.sync.dma_start(w4_sc_raw[loaded_rows, :], w4_scales.rearrange("a q c -> (a q) c").bitcast(I32))
        first_words = table.tile([P, T], I32, name="tab0", offset=TABLE_AT, align_bytes=ALIGN)
        tab_first = load_table(0, first_words)
        second_words = table.tile([P, T], I32, name="tab1", offset=SECOND_AT, align_bytes=ALIGN)
        tab_second = load_table(1, second_words)

        def pick_scales(j0, at):
            picked = staged.tile([P, HALF // WORD], I32, name="picked%d" % j0, offset=at, align_bytes=ALIGN)
            entries = idx[:, j0 // LIST_ROWS : (j0 + HALF) // LIST_ROWS]
            nc.vector.tensor_copy(picked[:].bitcast(U8), tab_sc[:].bitcast(U8).indirect(entries))
            return picked

        picked_lower = pick_scales(0, HALF - ALIGN)
        rows = keep.tile([P, (H + HALF) // WORD], I32, name="rows", align_bytes=ALIGN)
        nc.vector.tensor_copy(
            rows[:, 0 : H // WORD].rearrange("p (t g) -> p t g", t=PACK),
            w4_sc_raw[:].rearrange("p (g t) -> p t g", t=PACK),
        )
        nc.vector.tensor_copy(rows[:, H // WORD :], picked_lower[:])
        picked_upper = pick_scales(HALF, 0)

        def move_scale_rows(a, plane, source):
            start = ROWS_AT + ROWS_STEP * BLOCKS * a
            for r in range(QUAD_ROWS):
                of_row = slice(start + ROWS_STEP * r, start + ROWS_STEP * BLOCKS, ROWS_STEP * QUAD_ROWS)
                nc.sync.dma_start(plane[r:P:QUAD, :], source[of_row, :])

        plane_first = planes[:, 0 : (H + HALF) // WORD]
        plane_second = planes[:, (H + HALF) // WORD :]
        move_scale_rows(0, plane_first, rows)
        late_raw = staged.tile([P, PASSES * PACK * H], F32, name="w1_raw", offset=S - 2 * ALIGN, align_bytes=ALIGN)
        w1_0 = load_w1(late_raw[:, 0 : 4 * H], 0, 0, H)
        move_scale_rows(1, plane_second, rows)
        w1_10 = load_w1(late_raw[:, 4 * H : 6 * H], 1, 0, H // 2)
        w1_11 = load_w1(late_raw[:, 6 * H : 8 * H], 1, H // 2, H // 2)

        w1_q = keep.tile([P, PASSES, H], U32, name="w1_q", align_bytes=ALIGN)
        w1_sc = keep.tile([P, PASSES, H], U8, name="w1_sc", align_bytes=ALIGN)

        def quantise_w1(a, raw, first, width, on_scalar):
            rounded = [
                keep.tile([P, width * PACK], BF16, name="w1_bf%d%d_%d" % (a, first, t), align_bytes=ALIGN)
                for t in range(PACK)
            ]
            for t in range(PACK):
                grouped = rounded[t][:].rearrange("p (g l i) -> p g i l", l=LINE, i=PACK)
                if t in on_scalar:
                    nc.scalar.activation(grouped, raw[:, t], ACT.Copy, scale=-1.0)
                else:
                    nc.vector.tensor_scalar(grouped, raw[:, t], -1.0, None, MULT)
            for t in range(PACK):
                features = slice(t * P + first, t * P + first + width)
                nc.vector.quantize_mx(
                    out=w1_q[:, a, features].bitcast(FP8X4), scales=w1_sc[:, a, features], in_=rounded[t][:]
                )

        windows = []

        def new_window(pool):
            window = pool.tile([P, T2], F32, name="window%d" % len(windows), offset=0, align_bytes=ALIGN)
            nc.vector.memset(window[:], 0.0)
            windows.append(window)

        w4_q = keep.tile([P, PASSES, H // 2], I32, name="w4_q", align_bytes=ALIGN)
        for a in range(PASSES):
            nc.vector.tensor_copy(
                w4_q[:, a, :].rearrange("p (t g w) -> p t g w", t=PACK, w=LINE // 2),
                w4_raw[:, a, :].rearrange("p (g t w) -> p t g w", t=PACK, w=LINE // 2),
            )
        new_window(first_out)
        new_window(second_out)
        new_window(scale)

        v_q = {}

        def pick_words(a, j0, words_of, tag, width):
            words = keep.tile([P, width], U32, name="v_q%d_%d" % (a, j0), tag=tag, align_bytes=ALIGN)
            nc.vector.tensor_copy(words[:], words_of.indirect(idx[:, j0 // LIST_ROWS : (j0 + width) // LIST_ROWS]))
            for j in range(j0, j0 + width, COLS):
                v_q[a, j] = words[:, j - j0 : j - j0 + COLS]

        pick_words(0, 0, tab_first, "v_q00", HALF)
        pick_words(0, HALF, tab_first, "v_q02", HALF)
        windows.append(windows[0])

        w2_rows = w2.rearrange("(g t l) n -> t g l n", t=PACK, l=LINE)
        early = EARLY_TILES * P
        w2_early = table.tile([P, PACK, early], F32, name="w2_early", offset=9 * KB, align_bytes=ALIGN)
        wgo_sb = table.tile([P, S], F32, name="wgo_sb", offset=13 * KB, align_bytes=ALIGN)
        for t in range(PACK):
            nc.sync.dma_start(w2_early[:, t, :], w2_rows[t][:, :, 0:early])
        nc.sync.dma_start(wgo_sb[:], wgo)
        plane_late = table.tile([P, S // WORD], I32, name="plane_late", offset=8 * KB, align_bytes=ALIGN)
        nc.vector.memset(plane_late[:], 0)
        for a in range(PASSES):
            move_scale_rows(a, plane_late[:, a * HALF // WORD : (a + 1) * HALF // WORD], picked_upper)

        pick_words(1, 0, tab_second, "v_q10", HALF)
        pick_words(1, HALF, tab_second, "v_q12", HALF)
        quantise_w1(0, w1_0, 0, P, (2, 3))
        quantise_w1(1, w1_10, 0, P // 2, (3,))
        quantise_w1(1, w1_11, P // 2, P // 2, (3,))
        w2_late = table.tile([P, PACK, N - early], F32, name="w2_late", offset=SECOND_AT, align_bytes=ALIGN)
        for t in range(PACK):
            nc.sync.dma_start(w2_late[:, t, :], w2_rows[t][:, :, early:N])
        w4_scale_bytes = [plane.bitcast(U8)[:, 0:H] for plane in (plane_first, plane_second)]

        def v_scale_bytes(a, j0):
            if j0 >= HALF:
                return plane_late[:].bitcast(U8)[:, (a - 1) * HALF + j0 : (a - 1) * HALF + j0 + COLS]
            return (plane_first, plane_second)[a].bitcast(U8)[:, H + j0 : H + j0 + COLS]

        w2_q = keep.tile([P, N], U32, name="w2_q", align_bytes=ALIGN)
        w2_sc = keep.tile([P, N], U8, name="w2_sc", align_bytes=ALIGN)

        def round_w2(first, width, raw, on_scalar):
            tile = keep.tile([P, width, PACK], BF16, name="w2_bf%d" % first, align_bytes=ALIGN)
            if on_scalar:
                nc.scalar.activation(tile[:], raw.rearrange("p t n -> p n t"), ACT.Copy)
            else:
                nc.vector.tensor_copy(
                    tile[:].rearrange("p (c n) t -> p c t n", n=LINE), raw.rearrange("p t (c n) -> p c t n", n=LINE)
                )
            return tile

        def quantise_w2(first, width, tile):
            heads = slice(first, first + width)
            nc.vector.quantize_mx(
                out=w2_q[:, heads].bitcast(FP8X4), scales=w2_sc[:, heads], in_=tile[:].rearrange("p n t -> p (n t)")
            )

        w2_rounded = round_w2(0, early, w2_early[:], False)

        h_bf = {}
        for j0 in range(0, S, COLS):
            if j0 < HALF or j0 % CHUNK == 0:
                width = COLS if j0 < HALF else CHUNK
                if j0 == HALF - COLS:
                    tile = chain.tile([P, width, PACK], BF16, name="h_bf%d" % j0, offset=0, align_bytes=ALIGN)
                else:
                    tile = keep.tile([P, width, PACK], BF16, name="h_bf%d" % j0, align_bytes=ALIGN)
                first = j0
            h_bf[j0] = (tile, j0 - first)
        h_q = keep.tile([P, S], U32, name="h_q", align_bytes=ALIGN)
        h_sc = table.tile([P, S], U8, name="h_sc", offset=9 * KB, align_bytes=ALIGN)

        def square_differences(j0):
            bank = j0 // COLS
            diff = banks.tile([P, PACK, COLS], F32, name="diff%d" % bank, tag="bank%d" % bank)
            for step, (online, a) in enumerate(STEPS[j0 // CHUNK]):
                values = range(PACK) if j0 == 0 else reversed(range(PACK))
                for count, t in enumerate(values):
                    if online:
                        codes = w1_q[:, a, t * P : (t + 1) * P].bitcast(FP8X4)
                        scales = w1_sc[:, a, t * P : (t + 1) * P]
                    else:
                        codes = w4_q[:, a, t * P // 2 : (t + 1) * P // 2].bitcast(U8).bitcast(FP4X4)
                        scales = w4_scale_bytes[a][:, t * P : (t + 1) * P]
                    nc.tensor.matmul_mx(
                        diff[:, t, :],
                        lhsT=codes,
                        lhsT_scale=scales,
                        rhs=v_q[a, j0].bitcast(FP8X4),
                        rhs_scale=v_scale_bytes(a, j0),
                        start=(step == 0 and count == 0),
                        stop=(step == 2 * PASSES - 1 and count == PACK - 1),
                    )
            tile, first = h_bf[j0]
            nc.scalar.activation(tile[:, first : first + COLS, :], diff[:].rearrange("p t j -> p j t"), ACT.Square)

        def quantise_h(j0, width):
            cols = slice(j0, j0 + width)
            nc.vector.quantize_mx(
                out=h_q[:, cols].bitcast(FP8X4),
                scales=h_sc[:, cols],
                in_=h_bf[j0][0][:].rearrange("p j t -> p (j t)"),
            )

        ys = [keep.tile([P, S], F32, name="y%d" % n, align_bytes=ALIGN) for n in range(N // P)]
        second_y = chain.tile([P, CHUNK], F32, name="second_y", offset=KB, align_bytes=ALIGN)

        def y_of(n, j0, width):
            return second_y[:] if (n, j0) == (1, 0) else ys[n][:, j0 : j0 + width]

        def score(n, j0, width, bank):
            cols = slice(j0, j0 + width)
            heads = slice(n * P, (n + 1) * P)
            x = banks.tile([P, width], F32, name="x%d_%d" % (n, j0), tag="bank%d" % bank)
            nc.tensor.matmul_mx(
                x[:],
                lhsT=w2_q[:, heads].bitcast(FP8X4),
                lhsT_scale=w2_sc[:, heads],
                rhs=h_q[:, cols].bitcast(FP8X4),
                rhs_scale=h_sc[:, cols],
                start=True,
                stop=True,
            )
            nc.scalar.activation(y_of(n, j0, width), x[:], ACT.Sqrt, bias=first_one if n == 0 and j0 < CHUNK else one[:])

        def place(n, j0, width):
            places = idx2[:, j0 // LIST_ROWS : (j0 + width) // LIST_ROWS]
            nc.vector.tensor_tensor(
                windows[n][:].indirect(places), y_of(n, j0, width), wgo_sb[:, j0 : j0 + width], MULT
            )
            if j0 + width == S:
                nc.sync.dma_start(out[n * P : (n + 1) * P, :], windows[n][:])

        for j0 in range(0, CHUNK, COLS):
            square_differences(j0)
            quantise_h(j0, COLS)
            if j0 == 0:
                quantise_w2(0, early, w2_rounded)
        score(0, 0, COLS, 0)
        score(0, COLS, COLS, 1)
        for j0 in range(0, S, CHUNK):
            following = j0 + CHUNK
            if following < S:
                square_differences(following)
                square_differences(following + COLS)
            for n in range(EARLY_TILES):
                if n > 0 or j0 > 0:
                    score(n, j0, CHUNK, 2 if j0 == 0 else (following // COLS + n) % BANKS)
            place(0, j0, CHUNK)
            if following < S:
                step = COLS if following < HALF else CHUNK
                for j in range(following, following + CHUNK, step):
                    quantise_h(j, step)
            for n in range(1, EARLY_TILES):
                place(n, j0, CHUNK)

        quantise_w2(early, N - early, round_w2(early, N - early, w2_late[:], True))
        for n in range(EARLY_TILES, N // P):
            for j0 in range(0, S, HALF):
                score(n, j0, HALF, 2 + 2 * (j0 // HALF))
            place(n, 0, S)
